import numpy as np, ml_dtypes
CORES = [2,3,42,43,82,83,122,123]
N = 8
BF = ml_dtypes.bfloat16
def gentries(a):
    return np.ascontiguousarray(a.reshape(8, 16, -1).transpose(0, 2, 1)).reshape(8, -1)
def gtable(e):
    e = np.asarray(e); return np.ascontiguousarray(e.reshape(8, -1, 16).transpose(0, 2, 1)).reshape(128, -1).astype(np.int32)
W0, B, LN, RO, SP, CAP = 3072, 128, 2560, 4, 2, 768
W = W0 + RO * B
def parts(rng):
    scale = np.array([0.5, 1, 1.5, 2, 3, 4, 6, 8])[np.argsort(rng.random((N, 8)), axis=1)][:, :, None, None]; dens = 0.1 + 0.6 * rng.random((N, 8, 1, W0))
    cnt = np.where(rng.random((N, 8, 16, W0)) < dens, np.minimum(15, 1 + (scale * rng.standard_exponential((N, 8, 16, W0))).astype(np.int64)), 0)
    hot = rng.integers(0, W0, (N, 8, 64))
    def some(n, share):
        return np.where(rng.random((N, 8, n)) < share, np.take_along_axis(hot, rng.integers(0, 64, (N, 8, n)), 2), rng.integers(0, W0, (N, 8, n)))
    ptr = some(16 * W0, 0.4).reshape(N, 8, 16, W0); suf = (np.arange(W0) * rng.random((N, 8, W0))).astype(np.int64)
    return cnt, ptr, suf, rng.integers(0, W0, (N, 8, W0)), some(LN, 0.3), rng.integers(0, 256, (N, 8, RO * SP, LN))
def levels(rng, cnt, suf, v, g):
    x = np.arange(W0); b = np.where(x <= 16, 3, np.where(x <= 32, 2, np.where(x <= 48, 1, 0)))
    cnt[:, g] = np.where((np.arange(16) >> 2)[:, None] == b, rng.integers(1, 16, (N, 16, W0)), 0)
    suf[:, g] = rng.integers(1, 17, (N, W0)) + 16 * np.maximum(2 - b, 0)
    v[:, g, :SP - 1, :B] = rng.integers(240, 256, (N, SP - 1, B)); v[:, g, SP - 1, :B] = rng.integers(0, 128, (N, B))
def clones(rng, cnt, ptr, suf, lnk, cx, v, g):
    o = 1 + np.argsort(rng.random((N, W0 - 1)), axis=1); x = o[:, :B]; b = o[:, B:2 * B]; u = o[:, 2 * B:3 * B]
    qi = np.arange(N)[:, None]; z = rng.integers(1, 16, (N, B)); ct = cnt[:, g]; pt = ptr[:, g]
    for y in (x, u):
        ct[qi, :, y] = 0; ct[qi, 0, y] = 1; pt[qi, 0, y] = y
    ct[qi, :, b] = 0; ct[qi, z, b] = 1; pt[qi, z, b] = u
    suf[qi, g, x] = b; suf[qi, g, u] = x; lnk[qi, g, u] = np.maximum(lnk[qi, g, u], 1); cx[:, g, :B] = x
    v[:, g, :, :B] = rng.integers(0, 64, (N, RO * SP, B))
    for s in (SP - 2, 2 * SP - 2): v[:, g, s, :B] = rng.integers(128, 256, (N, B))
    if (RO - 2) * SP > 2:
        v[:, g, RO * SP - 2, :B] = rng.integers(64, 128, (N, B)); v[:, g, RO * SP - 1, :B] = rng.integers(128, 256, (N, B))
def kept(rng, cnt, ptr, suf, cx, v, g):
    o = 1 + np.argsort(rng.random((N, W0 - 1)), axis=1)[:, :(SP + 1) * B]; h = o[:, :SP * B]; b = o[:, SP * B:]
    qi = np.arange(N)[:, None]; z = rng.integers(1, 16, (N, B)); ct = cnt[:, g]; pt = ptr[:, g]
    ct[qi, :, h] = 0; ct[qi, 0, h] = 1; pt[qi, 0, h] = h; suf[qi, g, h] = o[:, B:]
    ct[qi, :, b] = 0; ct[qi, z, b] = 1; cx[:, g] = o[:, np.arange(LN) % B]
    v[:, g, :SP] = rng.integers(0, 128, (N, SP, LN)); v[1::2, g, SP - 1, :B] = rng.integers(128, 256, (N // 2, B))
    v[:, g, 2 * SP - 1, :B] = rng.integers(0, 128, (N, B))
def filled(rng, cnt, ptr, suf, lnk, cx, v, g):
    o = 1 + np.argsort(rng.random((N, W0 - 1)), axis=1)[:, :(2 * SP + 1) * B]; x = o[:, :B]; y = o[:, B:]; b1 = o[:, SP * B:(SP + 1) * B]; b2 = o[:, 2 * SP * B:]
    qi = np.arange(N)[:, None]; ct = cnt[:, g]; pt = ptr[:, g]
    ct[qi, :, o] = 0; ct[qi, 0, o] = 1; pt[qi, 0, o] = o
    for b, lo in ((b1, 1), (b2, 8)):
        ct[qi, 0, b] = 0; ct[qi, rng.integers(lo, lo + 7, (N, B)), b] = 1
    suf[qi, g, x] = np.roll(x, -1, axis=1); suf[qi, g, y[:, :-B]] = y[:, B:]; lnk[qi, g, x] = np.roll(y[:, :B], -1, axis=0)
    cx[:, g] = x[:, np.arange(LN) % B]
    v[:, g, :2 * SP] = rng.integers(0, 128, (N, 2 * SP, LN)); v[:, g, SP - 1, :B] = rng.integers(128, 256, (N, B))
    q4 = np.arange(N) % 4; v[:, g, 2 * SP - 1, :B // 2] += 128 * ((q4 == 1) | (q4 == 2))[:, None]
    if RO > 2: v[:, g, 3 * SP - 1, :B // 2] = rng.integers(0, 128, (N, B // 2))
def pack(cnt, ptr, suf, lnk, cx, v):
    return {"tab": np.ascontiguousarray((16 * ptr + cnt).reshape(N, 128, W0)).astype(np.int32), "suf": suf.astype(np.int32), "lnk": lnk.astype(np.int32),
            "cx": np.stack([gtable(a) for a in cx]), "vv": v.reshape(N, 8, RO * SP * LN).astype(np.float32).astype(BF)}
def setup_inputs(rng):
    return pack(*parts(rng))
def setup_inputs_room(rng):
    cnt, ptr, suf, lnk, cx, v = parts(rng)
    cnt = np.where(np.arange(16)[:, None] == rng.integers(0, 16, (N, 8, 1, W0)), np.maximum(cnt, 1), cnt); ptr = np.maximum(ptr, 1); cx = np.maximum(cx, 1)
    v[:, :, :SP - 1] = rng.integers(0, 128, (N, 8, SP - 1, LN)); opts = (0, 1, CAP - 1, CAP, CAP + 1, LN)
    for q in range(N):
        o = rng.permutation(6)
        for g in range(6):
            m = opts[g] if q == 0 else opts[5 - g] if q == 1 else opts[int(o[g])]
            v[q, g, SP - 1] = np.where(rng.permutation(LN) < m, rng.integers(240, 256, LN), rng.integers(0, 128, LN))
    for g in (6, 7):
        levels(rng, cnt, suf, v, g)
        for q in range(N): cx[q, g, :B] = 64 + rng.permutation(W0 - 64)[:B]
    return pack(cnt, ptr, suf, lnk, cx, v)
def setup_inputs_ties(rng):
    cnt, ptr, suf, lnk, cx, v = parts(rng)
    rows = np.array([4, 1, 2, 8, 1, 0, 16, 4, 8, 8, 16]); vals = np.array([3, 1, 1, 1, 15, 0, 15, 1, 3, 7, 3]); k = rng.integers(0, 11, (N, 8, W0))
    order = np.argsort(rng.random((N, 8, W0, 16)), axis=-1)
    cnt = np.where(order < rows[k][..., None], vals[k][..., None], 0).transpose(0, 1, 3, 2)
    v = np.where(rng.random(v.shape) < 0.6, 16 * rng.integers(0, 17, v.shape), 15 * rng.integers(0, 18, v.shape)) + np.where(rng.random(v.shape) < 0.6, 0, rng.integers(-1, 2, v.shape))
    return pack(cnt, ptr, suf, lnk, cx, np.minimum(np.maximum(v, 0), 255))
def setup_inputs_alike(rng):
    cnt, ptr, suf, lnk, cx, v = parts(rng); few = rng.integers(1, W0, (N, 8, 6))
    def some(n, m):
        return np.take_along_axis(few, rng.integers(0, m, (N, 8, n)), 2)
    ptr = some(16 * W0, 6).reshape(N, 8, 16, W0); suf = np.where(rng.random((N, 8, W0)) < 0.5, some(W0, 6), suf); lnk = np.where(rng.random((N, 8, W0)) < 0.5, some(W0, 6), lnk); cx = some(LN, 4)
    levels(rng, cnt, suf, v, 3); cx[:, 3, :B] = rng.choice(np.array([70, W0 - 1]), (N, B))
    cx[:, 5] = cx[:, 5, :1]; v[:, 5] = v[:, 5, :, :1]
    filled(rng, cnt, ptr, suf, lnk, cx, v, 2); kept(rng, cnt, ptr, suf, cx, v, 6); clones(rng, cnt, ptr, suf, lnk, cx, v, 7)
    return pack(cnt, ptr, suf, lnk, cx, v)
def setup_inputs_ends(rng):
    cnt, ptr, suf, lnk, cx, v = parts(rng); e = np.array([0, 1, W0 - 1])
    ptr = np.where(rng.random(ptr.shape) < 0.3, rng.choice(e, ptr.shape), ptr); lnk = np.where(rng.random(lnk.shape) < 0.5, rng.choice(e, lnk.shape), lnk); cx = np.where(rng.random(cx.shape) < 0.5, rng.choice(e, cx.shape), cx)
    suf[:, 1::2] = np.where(rng.random((N, 4, W0)) < 0.3, np.arange(W0), rng.integers(0, W0, (N, 4, W0))); suf[:, 2] = 0; suf[:, 4] = 0; suf[:, 5] = 0
    cnt[:, 4, :, 0] = 0; cnt[:, 5, :, 0] = 15; cnt[:, 6] = 15 * (cnt[:, 6] > 0); cnt[:, 7, :, W0 - 1] = 0; cnt[:, 0, :, W0 - 1] = 15
    v = np.where(rng.random(v.shape) < 0.7, rng.choice(np.array([0, 1, 127, 128, 239, 240, 254, 255]), v.shape), v)
    return pack(cnt, ptr, suf, lnk, cx, v)
def setup_inputs_spread(rng):
    def low(*shape):
        return np.minimum((W0 * rng.random(shape) ** rng.integers(1, 5, shape[:2] + (1,) * (len(shape) - 2))).astype(np.int64), W0 - 1)
    cnt = np.where(rng.random((N, 8, 16, W0)) < rng.random((N, 8, 1, W0)) ** 2, np.minimum(np.exp2(4 * rng.random((N, 8, 16, W0)) * rng.random((N, 8, 1, W0)) ** 0.5).astype(np.int64), 15), 0)
    v = np.minimum((256 * rng.random((N, 8, RO * SP, LN)) ** 3).astype(np.int64), 255)
    return pack(cnt, low(N, 8, 16, W0), low(N, 8, W0), W0 - 1 - low(N, 8, W0), low(N, 8, LN), np.where(rng.random(v.shape) < 0.5, v, 255 - v))
def check_inputs(d):
    bad = []
    for k, hi in (("tab", 16 * W0 - 1), ("suf", W0 - 1), ("lnk", W0 - 1), ("cx", W0 - 1)):
        if np.min(d[k]) < 0 or np.max(d[k]) > hi: bad.append("range of " + k)
    v = np.asarray(d["vv"]).astype(np.float32)
    if not np.all((v >= 0) & (v <= 255) & (v == np.floor(v))): bad.append("range of vv")
    return bad
def reference(tab, suf, lnk, cx, vv):
    k = tab.astype(np.int32).reshape(N, 8, 16, W0)
    C = np.zeros((N, 8, 16, W), np.int32); S = np.zeros((N, 8, 16, W), np.int32); C[..., :W0] = k & 15; S[..., :W0] = k >> 4
    F = np.zeros((N, 8, W), np.int32); L = np.zeros((N, 8, W), np.int32); F[..., :W0] = suf; L[..., :W0] = lnk
    v = vv.astype(np.float32).astype(np.int32).reshape(N, 8, RO, SP, 1, LN)
    c = np.stack([gentries(a) for a in cx]).astype(np.int32); e = np.zeros((N, 8, 16, LN), np.int32); f = np.full((N, 8, LN), -1, np.int32)
    qi = np.arange(N)[:, None, None]; gi = np.arange(8)[None, :, None]
    for t in range(RO):
        for s in range(SP):
            cc = np.take_along_axis(C, c[:, :, None, :], 3)
            n = cc * (1 - e); P = np.add.accumulate(n, axis=2, dtype=np.int32); E = np.add.reduce((n > 0).astype(np.int32), axis=2)
            z = np.add.reduce((256 * P <= v[:, :, t, s] * (P[:, :, 15] + E)[:, :, None, :]).astype(np.int32), axis=2)
            z = np.where(c == 0, np.minimum(z, 15), z); esc = z == 16
            d, fb = c, f
            f = np.where(esc, np.where(fb < 0, d, fb), -1)
            e = np.where(esc[:, :, None, :], np.maximum(e, (cc > 0).astype(np.int32)), 0)
            c = np.where(esc, F[qi, gi, d], S[qi, gi, np.minimum(z, 15), d])
        for q in range(N):
            for g in range(8):
                j = np.nonzero(~esc[q, g, :B] & (fb[q, g, :B] >= 0))[0]
                a = j[np.unique(fb[q, g, j], return_index=True)[1]]
                w = W0 + B * t + a; to = c[q, g, a]
                cw = (C[q, g][:, to] + 1) >> 1; sw = S[q, g][:, to]
                C[q, g][:, w] = cw; S[q, g][:, w] = sw; F[q, g, w] = to; L[q, g, w] = L[q, g, to]
                C[q, g, z[q, g, a], fb[q, g, a]] = 1; S[q, g, z[q, g, a], fb[q, g, a]] = w
                b = j[np.unique(d[q, g, j], return_index=True)[1]]
                C[q, g, z[q, g, b], d[q, g, b]] = np.minimum(15, C[q, g, z[q, g, b], d[q, g, b]] + 1)
        slot = esc & (np.add.accumulate(esc.astype(np.int32), axis=2) <= CAP)
        c2 = np.array(c); e2 = np.array(e); f2 = np.array(f)
        for r in range(N):
            q = (r - 1) % N
            for g in range(8):
                a = np.nonzero(slot[q, g])[0]; b = np.nonzero(slot[r, g])[0]; m = min(len(a), len(b)); a = a[:m]; b = b[:m]
                c2[r, g, b] = L[q, g, c[q, g, a]]; e2[r, g][:, b] = e[q, g][:, a]; f2[r, g, b] = -1
        c, e, f = c2, e2, f2
    return {"yn": C.reshape(N, 128, W).astype(np.float32).astype(BF), "yc": np.stack([gtable(a) for a in c]).astype(np.float32)}

@@ -1,0 +1,538 @@
+from concourse.mybir import dt, AluOpType as OP, ActivationFunctionType as AF
+
+EPS = 2.0 ** -14
+W0, B, LN, RO, SP, CAP = 3072, 128, 2560, 4, 2, 768
+W = W0 + RO * B
+WD = W + B
+XS = "AB"
+CQ = {"A": slice(0, 96), "B": slice(96, 160)}
+NQ = {"A": 96, "B": 64}
+PIECES = {"A": [0, 1, 2], "B": [3, 4]}
+
+_F, _H, _I, _B, _U = "float32", "float16", "int32", "bfloat16", "uint16"
+SCRATCH = {}
+for _n, _w, _d in (
+        ("tb", WD, _I), ("kt", WD, _F), ("dtb", WD, _F), ("gt", WD, _B), ("lt", WD, _B),
+        ("ci", 1024, _I), ("cb", 1024, _B), ("sg", 1024, _B), ("si", 1024, _I), ("s16", 1024, _H), ("rr", 1024, _I),
+        ("dn", 576, _I), ("dg", 1152, _I), ("dgb", 1152, _B), ("v1", 1280, _F), ("v31", 1280, _F),
+        ("iox", 160, _I), ("iop", 1, _I), ("ti", 160, _I), ("pi", 2, _I), ("xf", 160, _F), ("xg", 160, _F), ("xr", 160, _F),
+        ("pc", 32, _F), ("oh16", 16, _F), ("m32", 16, _F), ("jg", 160, _F), ("dj", 16, _F),
+        ("mats", 13 * 128, _B), ("sels", 5 * 160, _B), ("expa", 2048, _B), ("ones", 512, _B), ("tm1", 128, _F), ("tm2", 128, _F),
+        ("ca", 160, _I), ("cc", 160, _I), ("cl", 160, _U), ("pp", 160, _I), ("vs", 160, _F), ("wp", 160, _F), ("qq", 160, _H),
+        ("ff", 160, _F), ("mm", 160, _I), ("es", 160, _B), ("inc", 168, _F), ("zer", 96, _F), ("sa", 160, _F), ("sb2", 160, _F),
+        ("sl", 160, _U), ("rl", 160, _U), ("nr", 160, _F), ("c1", 160, _F), ("rc", 160, _F), ("yo", 160, _F), ("pw", 2 * LN, _B),
+        ("h0", 8, _F), ("h1", 8, _F), ("ht", 8, _F), ("hu", 8, _F), ("e8", 8, _F), ("cnd", 8, _F),
+        ("ka", 24, _F), ("k32", 24, _F), ("k16", 24, _H), ("fd", 16, _F), ("fdu", 16, _U), ("fy", 16, _F), ("lw", 16, _U),
+        ("kr", 256, _B), ("cr", 256, _B), ("ohb", 128, _B), ("ohf", 128, _F), ("oh3", 128, _F), ("o33", 128, _F),
+        ("chi", 128, _I), ("chf", 128, _F), ("cm", 128, _F), ("kf", 128, _F), ("k2", 128, _F), ("xi", 128, _I), ("xs", 128, _I),
+        ("xt", 128, _F), ("xw", 128, _F), ("rci", 128, _I), ("g1", 128, _B), ("gf", 128, _B), ("wdl", 128, _F), ("ynb", W, _B)):
+    SCRATCH[_n] = ("sbuf", [128, _w], _d)
+SCRATCH["vr"] = ("sbuf", [8, 20480], _B)
+SCRATCH["eq"] = ("sbuf", [128, 16, 128], _B)
+SCRATCH["msk"] = ("sbuf", [128, 16, 16], _B)
+for _x in XS:
+    for _n, _d in (("kap", _H), ("ds", _H), ("gg", _B), ("ne", _B), ("em", _B), ("cd", _B)):
+        SCRATCH[_n + _x] = ("sbuf", [128, 16 * NQ[_x]], _d)
+for _k in range(RO):
+    SCRATCH["rb%d" % _k] = ("sbuf", [128, CAP + 16], _B)
+for _k in range(8):
+    SCRATCH["b%d" % _k] = ("psum", [128, 512], _F)
+SEMAPHORES = ["cv", "ct", "cs", "cg"] + ["ld%d" % k for k in range(16)] + ["gd%d" % k for k in range(6)] + ["arr%d" % k for k in range(RO)] + ["snt%d" % k for k in range(RO)]
+
+
+def rank_program(g, core, T, topo):
+    rank = T.rank_of(core)
+    if rank is None:
+        return
+    E = {"v": g.vector, "t": g.tensor, "s": g.scalar, "g": g, "y": g.sync}
+    V, S, PE = g.vector, g.scalar, g.tensor
+    cnt, waited, lw, lr = {}, {}, {}, {}
+
+    def need(eng, sem, val):
+        if waited.get((eng, sem), 0) < val:
+            E[eng].wait_ge(T.sem[sem], val)
+            waited[(eng, sem)] = val
+
+    def deps(eng, r, w):
+        todo = {}
+        ds = [lw[k] for k in list(r) + list(w) if k in lw]
+        for k in w:
+            ds += list(lr.get(k, {}).values())
+        for d in ds:
+            if not (d[0] == eng == "t"):
+                todo[d[1]] = max(todo.get(d[1], 0), d[2])
+        for s in todo:
+            need(eng, s, todo[s])
+
+    def mark(d, r, w):
+        for k in w:
+            lw[k] = d
+            lr[k] = {}
+        for k in r:
+            if k not in w:
+                lr.setdefault(k, {})[d[1]] = d
+
+    def op(eng, fn, r="", w=""):
+        r = r.split()
+        w = w.split()
+        w = w + [k for k in r if len(k) == 2 and k[0] == "b" and k not in w]
+        deps(eng, r, w)
+        sem = "c" + eng
+        cnt[sem] = cnt.get(sem, 0) + 1
+        fn().then_inc(T.sem[sem], 1)
+        mark((eng, sem, cnt[sem]), r, w)
+
+    def dma(eng, out, in_, sem, r="", w=""):
+        r = r.split()
+        w = w.split()
+        deps(eng, r, w)
+        cnt[sem] = cnt.get(sem, 0) + 16
+        E[eng].dma_start(out, in_).then_inc(T.sem[sem], 16)
+        mark(("dma", sem, cnt[sem]), r, w)
+
+    def vts(out, in0, r, w, s1, o0, s2=None, o1=None):
+        if o1 is None:
+            op("v", lambda: V.tensor_scalar(out, in0, s1, None, o0), r, w)
+        else:
+            op("v", lambda: V.tensor_scalar(out, in0, s1, s2, o0, o1), r, w)
+
+    def vtt(out, a, b, r, w, alu):
+        op("v", lambda: V.tensor_tensor(out, a, b, alu), r, w)
+
+    def vcp(out, in_, r, w):
+        op("v", lambda: V.tensor_copy(out, in_), r, w)
+
+    def vset(out, c, w):
+        op("v", lambda: V.memset(out, c), "", w)
+
+    def act(out, in_, r, w, func, bias=0.0, scale=1.0):
+        op("s", lambda: S.activation(out, in_, func, bias=bias, scale=scale), r, w)
+
+    def mms(out, pairs, r, w):
+        def f():
+            for i, (a, b) in enumerate(pairs):
+                x = PE.matmul(out, a, b, i == 0, i == len(pairs) - 1)
+            return x
+        op("t", f, r, w)
+
+    for k in range(3):
+        dma("y", T.tb[:, 1024 * k:1024 * k + 1024], T.tab[:, 1024 * k:1024 * k + 1024], "ld%d" % k, "", "tb%d" % k)
+    dma("s", T.dn[:, 384:576], T.tab[0::16, :], "ld3", "", "dnt")
+    dma("s", T.dn[:, 0:192], T.suf[:, :], "ld4", "", "dnf")
+    dma("s", T.dn[:, 192:384], T.lnk[:, :], "ld5", "", "dnl")
+    dma("s", T.ca[:], T.cx[:, :], "ld6", "", "caA caB")
+    dma("s", T.vr[:, :], T.vv[:, :], "ld7", "", "vr")
+
+    op("g", lambda: g.iota(T.iop[:], [[1, 1]], 0, 1), "", "iop")
+    op("g", lambda: g.iota(T.iox[:], [[1, 160]], 0, 0), "", "iox")
+    vts(T.pi[:, 0:1], T.iop[:], "iop", "pi", 4, OP.arith_shift_right)
+    vts(T.pi[:, 1:2], T.iop[:], "iop", "pi1", 15, OP.bitwise_and)
+    PGC, PRC, PFC, P16, PM1, PP1, A1, A2, C15, WDc, WSc, WFc, R01, N15, D15, T1, T2 = range(17)
+
+    def col(i):
+        return T.pc[:, i:i + 1]
+
+    def key(i):
+        return "pc%d" % i
+    vcp(col(PGC), T.pi[:, 0:1], "pi", key(PGC))
+    vcp(col(PRC), T.pi[:, 1:2], "pi1", key(PRC))
+    vcp(col(PFC), T.iop[:], "iop", key(PFC))
+    vcp(T.xf[:], T.iox[:], "iox", "xf")
+    vts(T.oh16[:], T.xf[:, 0:16], "xf " + key(PRC), "oh16", col(PRC), OP.is_equal)
+
+    def ohc(i):
+        return T.oh16[:, i:i + 1]
+    names = ["ida", "idb", "idc", "mdf", "mfl", "blk", "tri", "i14", "n8k", "e15", "moh", "mz0", "mz1"]
+    M = {n: T.mats[:, 128 * i:128 * i + 128] for i, n in enumerate(names)}
+    M.update({n: T.sels[:, 160 * i:160 * i + 160] for i, n in enumerate(["selt", "seld", "selS", "selF", "vsel"])})
+    xm = T.xf[:, 0:128]
+
+    def mat(out, name, c, m, extra=""):
+        vts(out, xm, "xf " + key(c) + " " + extra, name, col(c), OP.is_equal, m, OP.mult)
+
+    def colop(i, src, srck, s1, o0, s2=None, o1=None):
+        vts(col(i), src, srck, key(i), s1, o0, s2, o1)
+    mat(M["ida"], "ida", PFC, 32.0)
+    mat(M["idb"], "idb", PFC, 1.0)
+    mat(M["idc"], "idc", PFC, EPS)
+    colop(PM1, col(PFC), key(PFC), 1.0, OP.subtract)
+    colop(A1, ohc(0), "oh16", -1.0 / 4096, OP.mult, 1.0 / 4096, OP.add)
+    colop(A2, ohc(15), "oh16", 1.0 / 4096, OP.mult, -1.0 / 4096, OP.add)
+    mat(T.tm1[:], "tm1", PM1, col(A1), key(A1))
+    mat(T.tm2[:], "tm2", PFC, col(A2), key(A2))
+    vtt(M["mdf"], T.tm1[:], T.tm2[:], "tm1 tm2", "mdf", OP.add)
+    vts(M["mfl"], M["idb"], "idb oh16", "mfl", ohc(15), OP.mult, 0.25, OP.mult)
+    vset(T.ones[:], 1.0, "ones")
+    colop(N15, ohc(15), "oh16", -1.0, OP.mult, 1.0, OP.add)
+    vset(T.gt[:], 0.0, "gtx gt0 gt1 gt2 gt3")
+    vset(T.lt[:], -2.0, "ltx lt0 lt1")
+    GT = "gtx gt0 gt1 gt2 gt3"
+    LT = "ltx lt0 lt1"
+    q = 192
+    vts(T.dg[:, 0:q], T.dn[:, 384:576], "dnt", "dg0", 4, OP.arith_shift_right, 63, OP.bitwise_and)
+    vts(T.dg[:, q:2 * q], T.dn[:, 384:576], "dnt", "dg1", 10, OP.arith_shift_right)
+    vts(T.dg[:, 2 * q:3 * q], T.dn[:, 0:192], "dnf", "dg2", 63, OP.bitwise_and)
+    vts(T.dg[:, 3 * q:4 * q], T.dn[:, 0:192], "dnf", "dg3", 6, OP.arith_shift_right)
+    vts(T.dg[:, 4 * q:5 * q], T.dn[:, 192:384], "dnl", "dg4", 63, OP.bitwise_and)
+    vts(T.dg[:, 5 * q:6 * q], T.dn[:, 192:384], "dnl", "dg5", 6, OP.arith_shift_right)
+    vcp(T.dgb[:, 0:4 * q], T.dg[:, 0:4 * q], "dg0 dg1 dg2 dg3", "dgb0")
+    vts(T.dgb[:, 4 * q:6 * q], T.dg[:, 4 * q:6 * q], "dg4 dg5", "dgb1", -1.0, OP.mult, -2.0, OP.add)
+    for k in range(4):
+        dma("y", T.gt[k::16, 0:W0], T.dgb[:, k * q:k * q + q], "gd%d" % k, "dgb0", "gt%d" % k)
+    for k in range(2):
+        dma("y", T.lt[k::16, 0:W0], T.dgb[:, (4 + k) * q:(5 + k) * q], "gd%d" % (4 + k), "dgb1", "lt%d" % k)
+
+    pb = [0]
+
+    def nextbank():
+        pb[0] += 1
+        return "b%d" % (pb[0] % 7)
+    for k in range(3):
+        c0 = 1024 * k
+        tbk = T.tb[:, c0:c0 + 1024]
+        vts(T.ci[:], tbk, "tb%d" % k, "ci", 15, OP.bitwise_and)
+        vcp(T.cb[:], T.ci[:], "ci", "cb")
+        act(T.sg[:], T.cb[:], "cb", "sg", AF.Sign)
+        for h in range(2):
+            p = slice(512 * h, 512 * h + 512)
+            bk = nextbank()
+            mms(T[bk][:], [(M["ida"], T.cb[:, p]), (M["idb"], T.sg[:, p]), (M["idc"], T.sg[:, p])], "ida idb idc cb sg", bk)
+            act(T.kt[:, c0 + 512 * h:c0 + 512 * h + 512], T[bk][:], bk, "kt%d%d" % (k, h), AF.Copy, bias=-EPS)
+        vts(T.si[:], tbk, "tb%d" % k, "si", 4, OP.arith_shift_right)
+        vts(T.s16[:], T.si[:], "si", "s16", 1792.0, OP.subtract)
+        for h in range(2):
+            p = slice(512 * h, 512 * h + 512)
+            bk = nextbank()
+            mms(T[bk][:], [(M["mdf"], T.s16[:, p]), (M["mfl"], T.ones[:])], "mdf mfl s16 ones", bk)
+            vcp(T.rr[:, p], T[bk][:], bk, "rr%d" % h)
+            vtt(T.dtb[:, c0 + 512 * h:c0 + 512 * h + 512], T[bk][:], T.rr[:, p], bk + " rr%d" % h, "dt%d%d" % (k, h), OP.subtract)
+    vts(T.dtb[:, 0:1], T.dtb[:, 0:1], "dt00 " + key(N15), "dt00", col(N15), OP.mult)
+    vset(T.kt[:, W0:WD], -EPS, "ktx")
+    KT = "ktx " + " ".join("kt%d%d" % (k, h) for k in range(3) for h in range(2))
+    DT = "dtx " + " ".join("dt%d%d" % (k, h) for k in range(3) for h in range(2))
+    TB = "tbx tb0 tb1 tb2"
+
+    vts(T.ti[:], T.iox[:], "iox", "ti", 4, OP.arith_shift_right)
+    vcp(T.xg[:], T.ti[:], "ti", "xg")
+    vts(T.ti[:], T.iox[:], "iox", "ti", 15, OP.bitwise_and)
+    vcp(T.xr[:], T.ti[:], "ti", "xr")
+    colop(P16, col(PGC), key(PGC), 16.0, OP.mult, 16.0, OP.add)
+    colop(PP1, col(PFC), key(PFC), 1.0, OP.add)
+    colop(C15, ohc(15), "oh16", 2.0 ** 25, OP.mult)
+    colop(WDc, ohc(15), "oh16", 2.0 ** 19 - 4096.0, OP.mult, 4096.0, OP.add)
+    colop(WSc, ohc(1), "oh16", 64.0, OP.mult, ohc(0), OP.add)
+    colop(WFc, ohc(3), "oh16", 64.0, OP.mult, ohc(2), OP.add)
+    colop(R01, ohc(0), "oh16", ohc(1), OP.add)
+    colop(D15, ohc(15), "oh16", 10.25, OP.mult, -10.0, OP.add)
+    colop(T1, col(PFC), key(PFC), 16.0, OP.mult, 16.0, OP.add)
+    colop(T2, col(PRC), key(PRC), 2560.0, OP.add)
+    vts(M["vsel"], T.xf[:], "xf " + key(T1), "vsel", col(T1), OP.is_equal)
+    vts(M["selt"], T.xf[:], "xf " + key(P16), "selt", col(P16), OP.is_equal)
+    for n, c in (("seld", WDc), ("selS", WSc), ("selF", WFc)):
+        vts(M[n], T.xf[:], "xf " + key(P16) + " " + key(c), n, col(P16), OP.is_equal, col(c), OP.mult)
+    vts(M["blk"], T.xg[:, 0:128], "xg " + key(PGC), "blk", col(PGC), OP.is_equal)
+    vts(T.tm1[:], T.xr[:, 0:128], "xr " + key(PRC), "tm1", col(PRC), OP.is_ge)
+    vtt(M["tri"], T.tm1[:], M["blk"], "tm1 blk", "tri", OP.mult)
+    vts(T.m32[:], T.oh16[:], "oh16", "m32", -32.0, OP.mult)
+    for r in range(16):
+        vts(T.expa[:, 128 * r:128 * r + 128], M["blk"], "blk m32", "expa%d" % r, T.m32[:, r:r + 1], OP.mult)
+    EXPA = " ".join("expa%d" % r for r in range(16))
+    mat(M["i14"], "i14", PFC, 2.0 ** 14)
+    vts(M["e15"], M["blk"], "blk " + key(C15), "e15", col(C15), OP.mult)
+
+    def late_constants():
+        vset(T.dtb[:, W0:WD], 0.0, "dtx")
+        vset(T.tb[:, W0:WD], 0, "tbx")
+        mat(M["n8k"], "n8k", PFC, -8192.0)
+        mat(T.tm1[:], "tm1", PP1, col(N15), key(N15))
+        mat(T.tm2[:], "tm2", PFC, col(N15), key(N15))
+        vtt(M["moh"], T.tm1[:], T.tm2[:], "tm1 tm2", "moh", OP.subtract)
+        mat(M["mz0"], "mz0", PFC, ohc(0), "oh16")
+        mat(T.tm1[:], "tm1", PP1, ohc(0), "oh16")
+        vtt(M["mz1"], T.tm1[:], M["mz0"], "tm1 mz0", "mz1", OP.add)
+        vts(T.jg[:], T.xf[:], "xf " + key(T2), "jg", 16.0, OP.mult, col(T2), OP.add)
+        for h in range(2):
+            vts(T.dj[:, 8 * h:8 * h + 8], T.jg[:, 0:8], "jg", "dj%d" % h, float(W - 2560), OP.add)
+        for h in range(16):
+            vts(T.msk[:, h, :], T.xr[:, 0:16], "xr " + key(PRC), "msk%d" % h, col(PRC), OP.is_gt)
+        vset(T.inc[:, 0:8], 8191.0, "inc0")
+        vset(T.zer[:], 0.0, "zer")
+        for k in range(RO):
+            vset(T["rb%d" % k][:, CAP:CAP + 16], 0.0, "rbx%d" % k)
+        vset(T.pw[:, 0:CAP], 0.0, "pw")
+        vts(T.xi[:], T.iox[:, 0:128], "iox", "xi", 63, OP.bitwise_and)
+        vts(T.xs[:], T.iox[:, 0:128], "iox", "xs", 6, OP.arith_shift_right)
+        vts(T.tm1[:], T.xi[:], "xi oh16", "tm1", ohc(0), OP.mult)
+        vts(T.tm2[:], T.xs[:], "xs oh16", "tm2", float(W0 // 64), OP.add, ohc(1), OP.mult)
+        vtt(T.wdl[:], T.tm1[:], T.tm2[:], "tm1 tm2", "wdl", OP.add)
+
+    def vlist(st):
+        mms(T.b7[:, 352:512], [(M["vsel"][0:8, 16 - r:144 - r], T.vr[0:8, st * LN + r:(st + 1) * LN:16]) for r in range(16)], "vsel vr", "b7")
+        act(T.v1[:, st * 160:st * 160 + 160], T.b7[:, 352:512], "b7", "v1_%d" % st, AF.Copy)
+        act(T.v31[:, st * 160:st * 160 + 160], T.b7[:, 352:512], "b7", "v31_%d" % st, AF.Copy, scale=31.0)
+
+    CUR = ["ca"]
+    HCUR = ["h0"]
+    for X in XS:
+        vcp(T.cl[:, CQ[X]], T.ca[:, CQ[X]], "ca" + X, "cl" + X)
+    vset(T.h0[:], 0.0, "h0")
+    vlist(0)
+
+    def selmm(out, w, base, rhs, rk, start=True, stop=True):
+        def f():
+            for r in range(16):
+                x = PE.matmul(out, M[base][:, 16 - r:144 - r], rhs[:, r::16], start and r == 0, stop and r == 15)
+            return x
+        op("t", f, base + " " + rk, w)
+
+    def pieces(X):
+        for i, b in enumerate(PIECES[X]):
+            yield "b%d" % b, slice(512 * i, 512 * i + 512), slice(CQ[X].start + 32 * i, CQ[X].start + 32 * i + 32)
+
+    def do_step(t, s):
+        st = 2 * t + s
+        wn = W0 + B * t
+        old = CUR[0]
+        new = "cc" if old == "ca" else "ca"
+        hold = HCUR[0]
+        hnew = "h1" if hold == "h0" else "h0"
+        tbank = {"A": "b7", "B": "b6"}
+        for X in XS:
+            kw = T.kt[:, 0:wn].indirect(T.cl[:, CQ[X]])
+            if st == 0:
+                vcp(T["kap" + X][:], kw, KT + " cl" + X, "kap" + X)
+            else:
+                vtt(T["kap" + X][:], kw, T["ne" + X][:], KT + " cl" + X + " ne" + X, "kap" + X, OP.mult)
+        if st == 0:
+            late_constants()
+        for X in XS:
+            act(T["gg" + X][:], T.gt[:, 0:wn].indirect(T.cl[:, CQ[X]]), GT + " cl" + X, "gg" + X, AF.Copy)
+        for X in XS:
+            c = CQ[X]
+            tk = tbank[X]
+            tp = T[tk][:, 0:NQ[X]]
+            selmm(tp, tk, "selt", T["kap" + X], "kap" + X)
+            vts(T.pp[:, c], tp, tk, "pp" + X, 1.0 / 32, OP.mult, 0.25, OP.subtract)
+            sc = slice(st * 160 + c.start, st * 160 + c.stop)
+            vtt(T.vs[:, c], tp, T.v1[:, sc], tk + " v1_%d" % st, "vs" + X, OP.mult)
+            vtt(T.wp[:, c], T.pp[:, c], T.v31[:, sc], "pp" + X + " v31_%d" % st, "wp" + X, OP.mult)
+            vtt(T.vs[:, c], T.vs[:, c], T.wp[:, c], "vs" + X + " wp" + X, "vs" + X, OP.subtract)
+            vts(T.qq[:, c], T.vs[:, c], "vs" + X, "qq" + X, 1.0 / 256, OP.mult, 1024.0 - 127.5 / 256, OP.add)
+        for X in XS:
+            for bk, p, cq in pieces(X):
+                def f(bk=bk, p=p, cq=cq, X=X):
+                    PE.matmul(T[bk][:], M["tri"], T["kap" + X][:, p], True, False)
+                    for r in range(16):
+                        x = PE.matmul(T[bk][:, r::16], T.expa[:, 128 * r:128 * r + 128], T.qq[:, cq], False, r == 15)
+                    return x
+                op("t", f, "tri kap" + X + " qq" + X + " " + EXPA, bk)
+                act(T["cd" + X][:, p], T[bk][:], bk, "cd" + X, AF.Sigmoid, bias=-16.0 * (32768 - 24), scale=-16.0)
+            if X == "A":
+                for Z in XS:
+                    selmm(T.b6[:, 64 + CQ[Z].start:64 + CQ[Z].stop], "b6", "selF", T["gg" + Z], "gg" + Z)
+                act(T.ff[:], T.b6[:, 64:224], "b6", "ff", AF.Copy, bias=65536.0)
+        for X in XS:
+            vtt(T["ds" + X][:], T.dtb[:, 0:wn].indirect(T.cl[:, CQ[X]]), T["cd" + X][:], DT + " cl" + X + " cd" + X, "ds" + X, OP.mult)
+        for X in XS:
+            c = CQ[X]
+            ap = T.b5[:, 0:NQ[X]]
+            selmm(ap, "b5", "selS", T["gg" + X], "gg" + X, True, False)
+            selmm(ap, "b5", "seld", T["ds" + X], "ds" + X, False, True)
+            vtt(T.mm[:, c], ap, T.ff[:, c], "b5 ff", "mm" + X, OP.min)
+            if X == "A":
+                vts(T.e8[:], T.b5[:, 0:8], "b5", "e8", 70000.0, OP.is_gt)
+            if s == 1:
+                vts(T.es[:, c], ap, "b5", "es" + X, 70000.0, OP.is_gt)
+            vts(T[new][:, c], T.mm[:, c], "mm" + X, new + X, 4095, OP.bitwise_and)
+            vcp(T.cl[:, c], T[new][:, c], new + X, "cl" + X)
+            if s == 1:
+                act(T["gg" + X][:], T.lt[:, 0:wn].indirect(T.cl[:, c]), LT + " cl" + X, "gg" + X, AF.Copy)
+                mms(T.b7[:, c], [(M["tri"], T.es[:, c]), (M["n8k"], T.es[:, c])], "tri n8k es" + X, "b7")
+                mms(T.b6[:, 0:NQ[X]], [(M["blk"], T.es[:, c])], "blk es" + X, "b6")
+            if s == 0 or t < RO - 1:
+                for bk, p, cq in pieces(X):
+                    mms(T[bk][:], [(M["i14"], T["kap" + X][:, p]), (M["e15"], T["ds" + X][:, p])], "i14 e15 kap" + X + " ds" + X, bk)
+                    if s == 0:
+                        act(T["ne" + X][:, p], T[bk][:], bk, "ne" + X, AF.Sigmoid, bias=256.0 * (2.0 ** 23 - 0.5), scale=-256.0)
+                    else:
+                        act(T["em" + X][:, p], T[bk][:], bk, "em" + X, AF.Sign, bias=-(2.0 ** 23 - 0.5))
+            if s == 1:
+                o = c.start
+                ik = "inc0" if X == "A" else "incA"
+                op("v", lambda: V.tensor_tensor_scan(T.inc[:, 8 + c.start:8 + c.stop], T.b6[:, 0:NQ[X]], T.zer[:, 0:NQ[X]], T.inc[:, 7 + o:8 + o], OP.add, OP.add), "b6 zer " + ik, "inc" + X)
+                vtt(T.sa[:, c], T.inc[:, 7 + c.start:7 + c.stop], T.b7[:, c], "b7 inc" + X + " " + ik, "sa" + X, OP.add)
+                vtt(T.sb2[:, c], T.sa[:, c], T.jg[:, c], "jg sa" + X, "sb" + X, OP.min)
+                vcp(T.sl[:, c], T.sb2[:, c], "sb" + X, "sl" + X)
+                vts(T.rl[:, c], T.sa[:, c], "sa" + X, "rl" + X, float(CAP), OP.min)
+        if st + 1 < RO * SP:
+            vlist(st + 1)
+        if s == 1:
+            send(t)
+        vts(T.ht[:], T[hold][:], hold, "ht", 0.0, OP.is_equal)
+        vts(T.hu[:], T[old][:, 0:8], old + "A", "hu", 1.0, OP.add)
+        vtt(T.ht[:], T.ht[:], T.hu[:], "ht hu", "ht", OP.mult)
+        vtt(T.ht[:], T.ht[:], T[hold][:], "ht " + hold, "ht", OP.add)
+        vtt(T[hnew][:], T.ht[:], T.e8[:], "ht e8", hnew, OP.mult)
+        CUR[0] = new
+        HCUR[0] = hnew
+        return old, hold
+
+    def send(t):
+        for X in XS:
+            pwi = T.pw[:].indirect(T.sl[:, CQ[X]])
+            if t < RO - 1:
+                vtt(pwi, T["gg" + X][:], T["em" + X][:], "sl" + X + " gg" + X + " em" + X, "pw", OP.mult)
+            else:
+                vcp(pwi, T["gg" + X][:], "sl" + X + " gg" + X, "pw")
+        deps("g", ["pw"], [])
+        dst = T.cores[(rank + 1) % len(T.cores)]
+        src = T.cores[(rank - 1) % len(T.cores)]
+        rid, pid, _se = topo.addr(dst)
+        g.remote_dma(T["rb%d" % t][:, 0:CAP], T.pw[:, 0:CAP], T.sem["arr%d" % t], T.sem["snt%d" % t], pid, rid, topo.mask(core, dst))
+        cnt["snt%d" % t] = len(topo.engines(core, dst))
+        cnt["arr%d" % t] = len(topo.engines(src, core))
+        mark(("rem", "snt%d" % t, cnt["snt%d" % t]), ["pw"], [])
+        lw["rb%d" % t] = ("rem", "arr%d" % t, cnt["arr%d" % t])
+
+    def hop_recv(t):
+        cur = CUR[0]
+        new = "cc" if cur == "ca" else "ca"
+        RB = "rb%d rbx%d" % (t, t)
+        win = T["rb%d" % t][:, 0:CAP + 16]
+        for X in XS:
+            act(T["gg" + X][:], win.indirect(T.rl[:, CQ[X]]), RB + " rl" + X, "gg" + X, AF.Abs)
+        if t < RO - 1:
+            for X in XS:
+                vtt(T["ne" + X][:], win.indirect(T.rl[:, CQ[X]]), T["em" + X][:], RB + " rl" + X + " em" + X, "ne" + X, OP.is_gt)
+        for X in XS:
+            c = CQ[X]
+            bp = T.b6[:, 0:NQ[X]]
+            selmm(bp, "b6", "selS", T["gg" + X], "gg" + X)
+            vts(T.nr[:, c], bp, "b6", "nr" + X, 1.0, OP.is_lt)
+            vts(T.rc[:, c], bp, "b6", "rc" + X, 130.0, OP.subtract, 0.0, OP.max)
+            vtt(T.c1[:, c], T[cur][:, c], T.nr[:, c], cur + X + " nr" + X, "c1" + X, OP.mult)
+            if t < RO - 1:
+                vtt(T[new][:, c], T.c1[:, c], T.rc[:, c], "c1" + X + " rc" + X, new + X, OP.add)
+                vcp(T.cl[:, c], T[new][:, c], new + X, "cl" + X)
+            else:
+                vtt(T.yo[:, c], T.c1[:, c], T.rc[:, c], "c1" + X + " rc" + X, "yo" + X, OP.add)
+        h = HCUR[0]
+        if t < RO - 1:
+            vtt(T[h][:], T[h][:], T.nr[:, 0:8], h + " nrA", h, OP.mult)
+        CUR[0] = new
+
+    def write_back(t, old, hb):
+        full = t < RO - 1
+        cur = CUR[0]
+        wn = W0 + B * t
+        wsl = slice(wn, wn + B)
+        l8 = T.cl[:, 0:8]
+        lf = T.fdu[:, 0:8]
+        vts(T.cnd[:], T[hb][:], hb, "cnd", 0.0, OP.is_gt)
+        vts(T.ht[:], T.e8[:], "e8", "ht", -1.0, OP.mult, 1.0, OP.add)
+        vtt(T.cnd[:], T.cnd[:], T.ht[:], "cnd ht", "cnd", OP.mult)
+        vts(T.ka[:, 0:8], T[hb][:], hb, "ka0", 3841.0, OP.subtract)
+        vts(T.ka[:, 8:16], T[old][:, 0:8], old + "A", "ka1", 3840.0, OP.subtract)
+        vts(T.ka[:, 16:24], T[cur][:, 0:8], cur + "A", "ka2", 3840.0, OP.subtract)
+        vts(T.fd[:], T.ka[:, 0:16], "ka0 ka1", "fd", 3840.0, OP.add, 0.0, OP.max)
+        vcp(T.fdu[:], T.fd[:], "fd", "fdu")
+        vtt(T.ka[:, 0:8], T.ka[:, 0:8], T.cnd[:], "ka0 cnd", "ka0", OP.mult)
+        vtt(T.ka[:, 8:16], T.ka[:, 8:16], T.cnd[:], "ka1 cnd", "ka1", OP.mult)
+        vts(T.k16[:], T.ka[:], "ka0 ka1 ka2", "k16", 2048.0, OP.add)
+        vts(T.k32[:], T.ka[:], "ka0 ka1 ka2", "k32", 2048.0, OP.add, -32.0, OP.mult)
+
+        def frow():
+            for r in range(16):
+                x = PE.matmul(T.b4[:, r:384:16], T.expa[:, 128 * r:128 * r + 128], T.k16[:], True, True)
+            return x
+        op("t", frow, EXPA + " k16", "b4")
+        mms(T.b5[:, 0:B], [(M["moh"], T.cdA[:, 0:B]), (M["mz0"], T.ones[:, 0:B])], "moh cdA mz0 ones", "b5")
+        act(T.ohf[:], T.b5[:, 0:B], "b5", "ohf", AF.Copy)
+        act(T.oh3[:], T.b5[:, 0:B], "b5", "oh3", AF.Copy, scale=32.0)
+        if full:
+            act(T.ohb[:], T.b5[:, 0:B], "b5", "ohb", AF.Copy)
+            act(T.g1[:], T.gt[:, 0:wn].indirect(l8), GT + " clA " + key(R01), "g1", AF.Copy, scale=col(R01))
+            act(T.gf[:], T.gt[:, 0:wn].indirect(lf), GT + " fdu", "gf", AF.Copy)
+            act(T.lt[:, wsl], T.lt[:, 0:wn].indirect(l8), LT + " clA", LT, AF.Copy)
+        for k in range(2):
+            for p in range(8):
+                i = 8 * k + p
+                vts(T.eq[:, i, 0:B - 16 * p], T.b4[:, B * k + 16 * p:B * k + B], "b4 k32", "eq%d" % i, T.k32[:, i:i + 1], OP.is_equal)
+        eqs = " ".join("eq%d" % i for i in range(16))
+        vtt(T.eq[:, :, 0:16], T.eq[:, :, 0:16], T.msk[:, :, :], eqs + " " + " ".join("msk%d" % h for h in range(16)), eqs, OP.mult)
+        vts(T.cr[:], T.b4[:, 0:256], "b4", "cr", -65536.0, OP.is_gt)
+
+        def fc():
+            for k in range(2):
+                for p in range(8):
+                    x = PE.matmul(T.b6[:, B * k + 16 * p:B * k + B], M["blk"], T.eq[:, 8 * k + p, 0:B - 16 * p], p == 0, p == 7)
+            return x
+        op("t", fc, "blk " + eqs, "b6")
+        djk = " dj0 dj1"
+        vts(T.chi[:], T.kt[:, 0:wn].indirect(l8), KT + " clA", "chi", 1.0 / 64, OP.mult, 0.25, OP.add)
+        vcp(T.kf[:], T.kt[:, 0:wn].indirect(lf), KT + " fdu", "kf")
+        vtt(T.fy[:], T.fd[:], T.dj[:], "fd" + djk, "fy", OP.subtract)
+        vts(T.fy[:], T.fy[:], "fy", "fy", 1.0 / 16, OP.mult)
+        vts(T.kr[:], T.b6[:, 0:256], "b6", "kr", 0.0, OP.is_equal)
+        vtt(T.kr[:], T.kr[:], T.cr[:], "kr cr", "kr", OP.mult)
+        selmm(T.b7[:, 0:16], "b7", "selt", T.kr, "kr")
+        vtt(T.chf[:], T.chi[:], T.kr[:, 0:B], "chi kr", "chf", OP.mult)
+        vts(T.cm[:], T.chf[:], "chf", "cm", 1.0, OP.min, 1.0 + EPS, OP.mult)
+        vts(T.chf[:], T.chf[:], "chf", "chf", 32.0, OP.mult, EPS, OP.subtract)
+        vts(T.k2[:], T.kf[:], "kf", "k2", -1.0, OP.mult, 33.0, OP.add)
+        vtt(T.k2[:], T.k2[:], T.ohf[:], "k2 ohf", "k2", OP.mult)
+        vts(T.o33[:], T.ohf[:], "ohf", "o33", 33.0 + EPS, OP.mult, EPS, OP.subtract)
+        vtt(T.fy[:], T.b7[:, 0:16], T.fy[:], "b7 fy", "fy", OP.mult)
+        vtt(T.fy[:], T.fy[:], T.dj[:], "fy" + djk, "fy", OP.add)
+        vcp(T.lw[:], T.fy[:], "fy", "lw")
+        vtt(T.kt[:, wsl], T.chf[:], T.cm[:], "chf cm", KT, OP.add)
+        vtt(T.kt[:].indirect(T.lw[:, 0:8]), T.kf[:], T.k2[:], "kf k2 lw", KT, OP.add)
+        if full:
+            vcp(T.xi[:], T.tb[:, 0:wn].indirect(lf), TB + " fdu", "xi")
+            vcp(T.tb[:, wsl], T.tb[:, 0:wn].indirect(l8), TB + " clA", TB)
+            vts(T.dtb[:, wsl], T.dtb[:, 0:wn].indirect(l8), DT + " clA " + key(D15), DT, col(D15), OP.max)
+            vts(T.xi[:], T.xi[:], "xi", "xi", 4, OP.arith_shift_right)
+            vts(T.xw[:], T.xf[:, 0:B], "xf", "xw", float(wn), OP.add)
+            vtt(T.xw[:], T.xw[:], T.xi[:], "xw xi", "xw", OP.subtract)
+            vtt(T.xw[:], T.xw[:], T.ohf[:], "xw ohf", "xw", OP.mult)
+            vtt(T.xw[:], T.xw[:], T.xi[:], "xw xi", "xw", OP.add)
+            vts(T.s16[:, 0:B], T.xw[:], "xw", "s16", 1792.0, OP.subtract)
+            mms(T.b5[:, 0:B], [(M["mdf"], T.s16[:, 0:B]), (M["mfl"], T.ones[:, 0:B])], "mdf mfl s16 ones", "b5")
+            vts(T.xs[:], T.xw[:], "xw", "xs", 16.0, OP.mult)
+            vcp(T.tb[:].indirect(T.lw[:, 0:8]), T.xs[:], "xs lw", TB)
+        vtt(T.k2[:], T.kt[:, 0:wn].indirect(T.fdu[:, 8:16]), T.oh3[:], KT + " fdu oh3", "k2", OP.add)
+        vts(T.k2[:], T.k2[:], "k2", "k2", 481.0, OP.min)
+        vtt(T.kt[:].indirect(T.lw[:, 8:16]), T.k2[:], T.o33[:], "k2 o33 lw", KT, OP.max)
+        if not full:
+            return
+        vcp(T.rr[:, 0:B], T.b5[:, 0:B], "b5", "rr0")
+        vtt(T.xt[:], T.b5[:, 0:B], T.rr[:, 0:B], "b5 rr0", "xt", OP.subtract)
+        vcp(T.dtb[:].indirect(T.lw[:, 0:8]), T.xt[:], "xt lw", DT)
+        mms(T.b6[:, 0:B], [(M["mz1"], T.ohb[:])], "mz1 ohb", "b6")
+        vts(T.rci[:], T.b4[:, 256:384], "b4", "rci", -1.0 / 32, OP.mult, 1792.0, OP.add)
+        vts(T.xi[:], T.rci[:], "rci", "xi", 63, OP.bitwise_and)
+        vts(T.xs[:], T.rci[:], "rci", "xs", 6, OP.arith_shift_right)
+        vts(T.xt[:], T.xi[:], "xi oh16", "xt", ohc(2), OP.mult)
+        vts(T.xw[:], T.xs[:], "xs oh16", "xw", ohc(3), OP.mult)
+        vtt(T.xt[:], T.xt[:], T.xw[:], "xt xw", "xt", OP.add)
+        vtt(T.gt[:, wsl], T.xt[:], T.g1[:], "xt g1", GT, OP.add)
+        vts(T.xw[:], T.ones[:, 0:B], "ones oh16", "xw", 2.0 * t, OP.mult, ohc(1), OP.mult)
+        vtt(T.xw[:], T.xw[:], T.wdl[:], "xw wdl", "xw", OP.add)
+        vtt(T.xw[:], T.xw[:], T.gf[:], "xw gf", "xw", OP.subtract)
+        vtt(T.g1[:], T.b6[:, 0:B], T.xw[:], "b6 xw", "g1", OP.mult)
+        vtt(T.gt[:].indirect(T.lw[:, 0:8]), T.gf[:], T.g1[:], "gf g1 lw", GT, OP.add)
+        vset(T.pw[:, 0:CAP], 0.0, "pw")
+
+    for t in range(RO):
+        do_step(t, 0)
+        old, hb = do_step(t, 1)
+        write_back(t, old, hb)
+        if t == RO - 1:
+            for h in range(2):
+                p = slice(W // 2 * h, W // 2 * (h + 1))
+                act(T.ynb[:, p], T.kt[:, p], KT, "yn%d" % h, AF.Relu, bias=-1.0 / 32, scale=1.0 / 32)
+                dma("y", T.yn[:, p], T.ynb[:, p], "ld%d" % (8 + h), "yn%d" % h, "")
+        hop_recv(t)
+    dma("y", T.yc[:, :], T.yo[:], "ld10", "yoA yoB", "")
+    for s in sorted(cnt):
+        need("g", s, cnt[s])

@@ -13,19 +13,20 @@ _F, _H, _I, _B, _U = "float32", "float16", "int32", "bfloat16", "uint16"
 SCRATCH = {}
 for _n, _w, _d in (
         ("tb", WD, _I), ("kt", WD, _F), ("dtb", WD, _F), ("gt", WD, _B), ("lt", WD, _B),
-        ("ci", 1024, _I), ("cb", 1024, _B), ("sg", 1024, _B), ("si", 1024, _I), ("s16", 1024, _H), ("rr", 1024, _I),
+        ("ci", 1024, _I), ("cb", 1024, _B), ("sg", 1024, _B), ("cb2", 1024, _B), ("sg2", 1024, _B), ("si", 1024, _I), ("s16", 1024, _H), ("rr", 1024, _I),
         ("dn", 576, _I), ("dg", 1152, _I), ("dgb", 1152, _B), ("v1", 1280, _F), ("v31", 1280, _F),
-        ("iox", 160, _I), ("iop", 1, _I), ("ti", 160, _I), ("pi", 2, _I), ("xf", 160, _F), ("xg", 160, _F), ("xr", 160, _F),
-        ("pc", 32, _F), ("oh16", 16, _F), ("m32", 16, _F), ("jg", 160, _F), ("dj", 16, _F),
-        ("mats", 13 * 128, _B), ("sels", 5 * 160, _B), ("expa", 2048, _B), ("ones", 512, _B), ("tm1", 128, _F), ("tm2", 128, _F),
+        ("iop", 1, _I), ("pi", 2, _I), ("xf", 160, _F), ("xg", 128, _F), ("xr", 128, _F),
+        ("pc", 32, _F), ("oh16", 16, _F), ("m32", 16, _F), ("jg", 160, _F), ("dja", 16, _F), ("djb", 16, _F),
+        ("mats", 14 * 128, _B), ("sels", 5 * 160, _B), ("expa", 2048, _B), ("ones", 512, _B), ("tm1", 128, _F), ("tm2", 128, _F), ("tm3", 128, _I),
         ("ca", 160, _I), ("cc", 160, _I), ("cl", 160, _U), ("pp", 160, _I), ("vs", 160, _F), ("wp", 160, _F), ("qq", 160, _H),
         ("ff", 160, _F), ("mm", 160, _I), ("es", 160, _B), ("inc", 168, _F), ("zer", 96, _F), ("sa", 160, _F), ("sb2", 160, _F),
         ("sl", 160, _U), ("rl", 160, _U), ("nr", 160, _F), ("c1", 160, _F), ("rc", 160, _F), ("yo", 160, _F), ("pw", 2 * LN, _B),
-        ("h0", 8, _F), ("h1", 8, _F), ("ht", 8, _F), ("hu", 8, _F), ("e8", 8, _F), ("cnd", 8, _F),
-        ("ka", 24, _F), ("k32", 24, _F), ("k16", 24, _H), ("fd", 16, _F), ("fdu", 16, _U), ("fy", 16, _F), ("lw", 16, _U),
-        ("kr", 256, _B), ("cr", 256, _B), ("ohb", 128, _B), ("ohf", 128, _F), ("oh3", 128, _F), ("o33", 128, _F),
+        ("h0", 8, _F), ("h1", 8, _F), ("ht", 8, _F), ("e8", 8, _F), ("cnd", 8, _F), ("dgi", 16, _I),
+        ("ka", 16, _F), ("k32", 16, _F), ("k16", 32, _H), ("fdu", 16, _U), ("fy", 16, _F), ("lw", 16, _U),
+        ("kr", 256, _B), ("cr", 256, _F), ("ohb", 128, _B), ("ohf", 128, _F), ("oh3", 128, _F), ("o33", 128, _F),
         ("chi", 128, _I), ("chf", 128, _F), ("cm", 128, _F), ("kf", 128, _F), ("k2", 128, _F), ("xi", 128, _I), ("xs", 128, _I),
-        ("xt", 128, _F), ("xw", 128, _F), ("rci", 128, _I), ("g1", 128, _B), ("gf", 128, _B), ("wdl", 128, _F), ("ynb", W, _B)):
+        ("xt", 128, _F), ("xw", 128, _F), ("xv", 128, _F), ("xd", 128, _F), ("wv", 128, _F), ("g1", 128, _B), ("g2", 128, _B), ("gf", 128, _B),
+        ("wdl", 128, _F), ("ynb", W, _B)):
     SCRATCH[_n] = ("sbuf", [128, _w], _d)
 SCRATCH["vr"] = ("sbuf", [8, 20480], _B)
 SCRATCH["eq"] = ("sbuf", [128, 16, 128], _B)
@@ -102,8 +103,8 @@ def rank_program(g, core, T, topo):
     def vcp(out, in_, r, w):
         op("v", lambda: V.tensor_copy(out, in_), r, w)
 
-    def vset(out, c, w):
-        op("v", lambda: V.memset(out, c), "", w)
+    def fill(out, pattern, base, w, cm=0):
+        op("g", lambda: g.iota(out, pattern, base, cm, allow_small_or_imprecise_dtypes=True), "", w)
 
     def act(out, in_, r, w, func, bias=0.0, scale=1.0):
         op("s", lambda: S.activation(out, in_, func, bias=bias, scale=scale), r, w)
@@ -117,32 +118,48 @@ def rank_program(g, core, T, topo):
 
     for k in range(3):
         dma("y", T.tb[:, 1024 * k:1024 * k + 1024], T.tab[:, 1024 * k:1024 * k + 1024], "ld%d" % k, "", "tb%d" % k)
+    dma("s", T.ca[:], T.cx[:, :], "ld6", "", "caA caB")
+    dma("s", T.vr[:, :], T.vv[:, :], "ld7", "", "vr")
     dma("s", T.dn[:, 384:576], T.tab[0::16, :], "ld3", "", "dnt")
     dma("s", T.dn[:, 0:192], T.suf[:, :], "ld4", "", "dnf")
     dma("s", T.dn[:, 192:384], T.lnk[:, :], "ld5", "", "dnl")
-    dma("s", T.ca[:], T.cx[:, :], "ld6", "", "caA caB")
-    dma("s", T.vr[:, :], T.vv[:, :], "ld7", "", "vr")
 
-    op("g", lambda: g.iota(T.iop[:], [[1, 1]], 0, 1), "", "iop")
-    op("g", lambda: g.iota(T.iox[:], [[1, 160]], 0, 0), "", "iox")
-    vts(T.pi[:, 0:1], T.iop[:], "iop", "pi", 4, OP.arith_shift_right)
-    vts(T.pi[:, 1:2], T.iop[:], "iop", "pi1", 15, OP.bitwise_and)
-    PGC, PRC, PFC, P16, PM1, PP1, A1, A2, C15, WDc, WSc, WFc, R01, N15, D15, T1, T2 = range(17)
+    PGC, PRC, PFC, P16, PM1, PP1, A1, A2, C15, WDc, WSc, WFc, R01, N15, D15, T1, T2, NPR, Q2, Q3, W2 = range(21)
 
     def col(i):
         return T.pc[:, i:i + 1]
 
     def key(i):
         return "pc%d" % i
+    fill(T.iop[:], [[1, 1]], 0, "iop", 1)
+    fill(col(PFC), [[1, 1]], 0, key(PFC), 1)
+    fill(T.xf[:], [[1, 160]], 0, "xf")
+    fill(T.xg[:], [[1, 8], [0, 16]], 0, "xg")
+    fill(T.xr[:], [[0, 8], [1, 16]], 0, "xr")
+    fill(T.ones[:], [[0, 512]], 1, "ones")
+    GT = "gtx gt0 gt1 gt2 gt3"
+    LT = "ltx lt0 lt1"
+    fill(T.dtb[:, W0:WD], [[0, WD - W0]], 0, "dtx")
+    fill(T.gt[:], [[0, WD]], 0, GT)
+    fill(T.lt[:], [[0, WD]], -2, LT)
+    fill(T.h0[:], [[0, 8]], 0, "h0")
+    fill(T.inc[:, 0:8], [[0, 8]], 8191, "inc0")
+    fill(T.zer[:], [[0, 96]], 0, "zer")
+    for k in range(RO):
+        fill(T["rb%d" % k][:, CAP:CAP + 16], [[0, 16]], 0, "rbx%d" % k)
+    fill(T.tb[:, W0:WD], [[0, WD - W0]], 0, "tbx")
+    fill(T.tm3[:], [[1, 128]], 0, "tm3")
+    fill(T.pw[:, 0:CAP], [[0, CAP]], 0, "pw")
+
+    vts(T.pi[:, 0:1], T.iop[:], "iop", "pi", 4, OP.arith_shift_right)
+    vts(T.pi[:, 1:2], T.iop[:], "iop", "pi1", 15, OP.bitwise_and)
     vcp(col(PGC), T.pi[:, 0:1], "pi", key(PGC))
     vcp(col(PRC), T.pi[:, 1:2], "pi1", key(PRC))
-    vcp(col(PFC), T.iop[:], "iop", key(PFC))
-    vcp(T.xf[:], T.iox[:], "iox", "xf")
     vts(T.oh16[:], T.xf[:, 0:16], "xf " + key(PRC), "oh16", col(PRC), OP.is_equal)
 
     def ohc(i):
         return T.oh16[:, i:i + 1]
-    names = ["ida", "idb", "idc", "mdf", "mfl", "blk", "tri", "i14", "n8k", "e15", "moh", "mz0", "mz1"]
+    names = ["ida", "idb", "idc", "mdf", "mfl", "blk", "tri", "i14", "n8k", "e15", "moh", "mz0", "mz1", "nhf"]
     M = {n: T.mats[:, 128 * i:128 * i + 128] for i, n in enumerate(names)}
     M.update({n: T.sels[:, 160 * i:160 * i + 160] for i, n in enumerate(["selt", "seld", "selS", "selF", "vsel"])})
     xm = T.xf[:, 0:128]
@@ -155,6 +172,17 @@ def rank_program(g, core, T, topo):
     mat(M["ida"], "ida", PFC, 32.0)
     mat(M["idb"], "idb", PFC, 1.0)
     mat(M["idc"], "idc", PFC, EPS)
+    vts(M["blk"], T.xg[:], "xg " + key(PGC), "blk", col(PGC), OP.is_equal)
+    vts(T.m32[:], T.oh16[:], "oh16", "m32", -32.0, OP.mult)
+    for r in range(16):
+        act(T.expa[:, 128 * r:128 * r + 128], M["blk"], "blk m32", "expa%d" % r, AF.Copy, scale=T.m32[:, r:r + 1])
+    EXPA = " ".join("expa%d" % r for r in range(16))
+    colop(T1, col(PFC), key(PFC), 16.0, OP.mult, 16.0, OP.add)
+    vts(M["vsel"], T.xf[:], "xf " + key(T1), "vsel", col(T1), OP.is_equal)
+    colop(P16, col(PGC), key(PGC), 16.0, OP.mult, 16.0, OP.add)
+    vts(M["selt"], T.xf[:], "xf " + key(P16), "selt", col(P16), OP.is_equal)
+    vts(T.tm1[:], T.xr[:], "xr " + key(PRC), "tm1", col(PRC), OP.is_ge)
+    vtt(M["tri"], T.tm1[:], M["blk"], "tm1 blk", "tri", OP.mult)
     colop(PM1, col(PFC), key(PFC), 1.0, OP.subtract)
     colop(A1, ohc(0), "oh16", -1.0 / 4096, OP.mult, 1.0 / 4096, OP.add)
     colop(A2, ohc(15), "oh16", 1.0 / 4096, OP.mult, -1.0 / 4096, OP.add)
@@ -162,25 +190,15 @@ def rank_program(g, core, T, topo):
     mat(T.tm2[:], "tm2", PFC, col(A2), key(A2))
     vtt(M["mdf"], T.tm1[:], T.tm2[:], "tm1 tm2", "mdf", OP.add)
     vts(M["mfl"], M["idb"], "idb oh16", "mfl", ohc(15), OP.mult, 0.25, OP.mult)
-    vset(T.ones[:], 1.0, "ones")
     colop(N15, ohc(15), "oh16", -1.0, OP.mult, 1.0, OP.add)
-    vset(T.gt[:], 0.0, "gtx gt0 gt1 gt2 gt3")
-    vset(T.lt[:], -2.0, "ltx lt0 lt1")
-    GT = "gtx gt0 gt1 gt2 gt3"
-    LT = "ltx lt0 lt1"
-    q = 192
-    vts(T.dg[:, 0:q], T.dn[:, 384:576], "dnt", "dg0", 4, OP.arith_shift_right, 63, OP.bitwise_and)
-    vts(T.dg[:, q:2 * q], T.dn[:, 384:576], "dnt", "dg1", 10, OP.arith_shift_right)
-    vts(T.dg[:, 2 * q:3 * q], T.dn[:, 0:192], "dnf", "dg2", 63, OP.bitwise_and)
-    vts(T.dg[:, 3 * q:4 * q], T.dn[:, 0:192], "dnf", "dg3", 6, OP.arith_shift_right)
-    vts(T.dg[:, 4 * q:5 * q], T.dn[:, 192:384], "dnl", "dg4", 63, OP.bitwise_and)
-    vts(T.dg[:, 5 * q:6 * q], T.dn[:, 192:384], "dnl", "dg5", 6, OP.arith_shift_right)
-    vcp(T.dgb[:, 0:4 * q], T.dg[:, 0:4 * q], "dg0 dg1 dg2 dg3", "dgb0")
-    vts(T.dgb[:, 4 * q:6 * q], T.dg[:, 4 * q:6 * q], "dg4 dg5", "dgb1", -1.0, OP.mult, -2.0, OP.add)
-    for k in range(4):
-        dma("y", T.gt[k::16, 0:W0], T.dgb[:, k * q:k * q + q], "gd%d" % k, "dgb0", "gt%d" % k)
-    for k in range(2):
-        dma("y", T.lt[k::16, 0:W0], T.dgb[:, (4 + k) * q:(5 + k) * q], "gd%d" % (4 + k), "dgb1", "lt%d" % k)
+    colop(WDc, ohc(15), "oh16", 2.0 ** 19 - 4096.0, OP.mult, 4096.0, OP.add)
+    colop(WSc, ohc(1), "oh16", 64.0, OP.mult, ohc(0), OP.add)
+    colop(WFc, ohc(3), "oh16", 64.0, OP.mult, ohc(2), OP.add)
+    for n, c in (("seld", WDc), ("selS", WSc), ("selF", WFc)):
+        vts(M[n], T.xf[:], "xf " + key(P16) + " " + key(c), n, col(P16), OP.is_equal, col(c), OP.mult)
+    colop(C15, ohc(15), "oh16", 2.0 ** 25, OP.mult)
+    mat(M["i14"], "i14", PFC, 2.0 ** 14)
+    vts(M["e15"], M["blk"], "blk " + key(C15), "e15", col(C15), OP.mult)
 
     pb = [0]
 
@@ -189,79 +207,75 @@ def rank_program(g, core, T, topo):
         return "b%d" % (pb[0] % 7)
     for k in range(3):
         c0 = 1024 * k
-        tbk = T.tb[:, c0:c0 + 1024]
-        vts(T.ci[:], tbk, "tb%d" % k, "ci", 15, OP.bitwise_and)
-        vcp(T.cb[:], T.ci[:], "ci", "cb")
-        act(T.sg[:], T.cb[:], "cb", "sg", AF.Sign)
+        cb, sg = ("cb", "sg") if k % 2 == 0 else ("cb2", "sg2")
+        vts(T.ci[:], T.tb[:, c0:c0 + 1024], "tb%d" % k, "ci", 15, OP.bitwise_and)
+        vcp(T[cb][:], T.ci[:], "ci", cb)
+        act(T[sg][:], T[cb][:], cb, sg, AF.Sign)
         for h in range(2):
             p = slice(512 * h, 512 * h + 512)
             bk = nextbank()
-            mms(T[bk][:], [(M["ida"], T.cb[:, p]), (M["idb"], T.sg[:, p]), (M["idc"], T.sg[:, p])], "ida idb idc cb sg", bk)
+            mms(T[bk][:], [(M["ida"], T[cb][:, p]), (M["idb"], T[sg][:, p]), (M["idc"], T[sg][:, p])], "ida idb idc " + cb + " " + sg, bk)
             act(T.kt[:, c0 + 512 * h:c0 + 512 * h + 512], T[bk][:], bk, "kt%d%d" % (k, h), AF.Copy, bias=-EPS)
-        vts(T.si[:], tbk, "tb%d" % k, "si", 4, OP.arith_shift_right)
-        vts(T.s16[:], T.si[:], "si", "s16", 1792.0, OP.subtract)
-        for h in range(2):
-            p = slice(512 * h, 512 * h + 512)
-            bk = nextbank()
-            mms(T[bk][:], [(M["mdf"], T.s16[:, p]), (M["mfl"], T.ones[:])], "mdf mfl s16 ones", bk)
-            vcp(T.rr[:, p], T[bk][:], bk, "rr%d" % h)
-            vtt(T.dtb[:, c0 + 512 * h:c0 + 512 * h + 512], T[bk][:], T.rr[:, p], bk + " rr%d" % h, "dt%d%d" % (k, h), OP.subtract)
-    vts(T.dtb[:, 0:1], T.dtb[:, 0:1], "dt00 " + key(N15), "dt00", col(N15), OP.mult)
-    vset(T.kt[:, W0:WD], -EPS, "ktx")
+    act(T.kt[:, W0:WD], T.dtb[:, W0:WD], "dtx", "ktx", AF.Copy, bias=-EPS)
     KT = "ktx " + " ".join("kt%d%d" % (k, h) for k in range(3) for h in range(2))
     DT = "dtx " + " ".join("dt%d%d" % (k, h) for k in range(3) for h in range(2))
     TB = "tbx tb0 tb1 tb2"
 
-    vts(T.ti[:], T.iox[:], "iox", "ti", 4, OP.arith_shift_right)
-    vcp(T.xg[:], T.ti[:], "ti", "xg")
-    vts(T.ti[:], T.iox[:], "iox", "ti", 15, OP.bitwise_and)
-    vcp(T.xr[:], T.ti[:], "ti", "xr")
-    colop(P16, col(PGC), key(PGC), 16.0, OP.mult, 16.0, OP.add)
-    colop(PP1, col(PFC), key(PFC), 1.0, OP.add)
-    colop(C15, ohc(15), "oh16", 2.0 ** 25, OP.mult)
-    colop(WDc, ohc(15), "oh16", 2.0 ** 19 - 4096.0, OP.mult, 4096.0, OP.add)
-    colop(WSc, ohc(1), "oh16", 64.0, OP.mult, ohc(0), OP.add)
-    colop(WFc, ohc(3), "oh16", 64.0, OP.mult, ohc(2), OP.add)
-    colop(R01, ohc(0), "oh16", ohc(1), OP.add)
-    colop(D15, ohc(15), "oh16", 10.25, OP.mult, -10.0, OP.add)
-    colop(T1, col(PFC), key(PFC), 16.0, OP.mult, 16.0, OP.add)
-    colop(T2, col(PRC), key(PRC), 2560.0, OP.add)
-    vts(M["vsel"], T.xf[:], "xf " + key(T1), "vsel", col(T1), OP.is_equal)
-    vts(M["selt"], T.xf[:], "xf " + key(P16), "selt", col(P16), OP.is_equal)
-    for n, c in (("seld", WDc), ("selS", WSc), ("selF", WFc)):
-        vts(M[n], T.xf[:], "xf " + key(P16) + " " + key(c), n, col(P16), OP.is_equal, col(c), OP.mult)
-    vts(M["blk"], T.xg[:, 0:128], "xg " + key(PGC), "blk", col(PGC), OP.is_equal)
-    vts(T.tm1[:], T.xr[:, 0:128], "xr " + key(PRC), "tm1", col(PRC), OP.is_ge)
-    vtt(M["tri"], T.tm1[:], M["blk"], "tm1 blk", "tri", OP.mult)
-    vts(T.m32[:], T.oh16[:], "oh16", "m32", -32.0, OP.mult)
-    for r in range(16):
-        vts(T.expa[:, 128 * r:128 * r + 128], M["blk"], "blk m32", "expa%d" % r, T.m32[:, r:r + 1], OP.mult)
-    EXPA = " ".join("expa%d" % r for r in range(16))
-    mat(M["i14"], "i14", PFC, 2.0 ** 14)
-    vts(M["e15"], M["blk"], "blk " + key(C15), "e15", col(C15), OP.mult)
+    def digits():
+        q = 192
+        vts(T.dg[:, 0:q], T.dn[:, 384:576], "dnt", "dg0", 4, OP.arith_shift_right, 63, OP.bitwise_and)
+        vts(T.dg[:, q:2 * q], T.dn[:, 384:576], "dnt", "dg1", 10, OP.arith_shift_right)
+        vts(T.dg[:, 2 * q:3 * q], T.dn[:, 0:192], "dnf", "dg2", 63, OP.bitwise_and)
+        vts(T.dg[:, 3 * q:4 * q], T.dn[:, 0:192], "dnf", "dg3", 6, OP.arith_shift_right)
+        vts(T.dg[:, 4 * q:5 * q], T.dn[:, 192:384], "dnl", "dg4", 63, OP.bitwise_and)
+        vts(T.dg[:, 5 * q:6 * q], T.dn[:, 192:384], "dnl", "dg5", 6, OP.arith_shift_right)
+        vcp(T.dgb[:, 0:4 * q], T.dg[:, 0:4 * q], "dg0 dg1 dg2 dg3", "dgb0")
+        vts(T.dgb[:, 4 * q:6 * q], T.dg[:, 4 * q:6 * q], "dg4 dg5", "dgb1", -1.0, OP.mult, -2.0, OP.add)
+        for k in range(4):
+            dma("y", T.gt[k::16, 0:W0], T.dgb[:, k * q:k * q + q], "gd%d" % k, "dgb0", "gt%d" % k)
+        for k in range(2):
+            dma("y", T.lt[k::16, 0:W0], T.dgb[:, (4 + k) * q:(5 + k) * q], "gd%d" % (4 + k), "dgb1", "lt%d" % k)
+
+    def pointers(k):
+        c0 = 1024 * k
+        vts(T.si[:], T.tb[:, c0:c0 + 1024], "tb%d" % k, "si", 4, OP.arith_shift_right)
+        vts(T.s16[:], T.si[:], "si", "s16", 1792.0, OP.subtract)
+        for h in range(2):
+            p = slice(512 * h, 512 * h + 512)
+            bk = "b%d" % (2 * (k % 2) + h)
+            mms(T[bk][:], [(M["mdf"], T.s16[:, p]), (M["mfl"], T.ones[:])], "mdf mfl s16 ones", bk)
+            vcp(T.rr[:, p], T[bk][:], bk, "rr%d" % h)
+            vtt(T.dtb[:, c0 + 512 * h:c0 + 512 * h + 512], T[bk][:], T.rr[:, p], bk + " rr%d" % h, "dt%d%d" % (k, h), OP.subtract)
+        if k == 0:
+            vts(T.dtb[:, 0:1], T.dtb[:, 0:1], "dt00 " + key(N15), "dt00", col(N15), OP.mult)
 
     def late_constants():
-        vset(T.dtb[:, W0:WD], 0.0, "dtx")
-        vset(T.tb[:, W0:WD], 0, "tbx")
+        colop(PP1, col(PFC), key(PFC), 1.0, OP.add)
+        colop(R01, ohc(0), "oh16", ohc(1), OP.add)
+        colop(D15, ohc(15), "oh16", 10.25, OP.mult, -10.0, OP.add)
+        colop(T2, col(PRC), key(PRC), 2560.0, OP.add)
+        colop(NPR, col(PRC), key(PRC), -1.0, OP.mult)
+        colop(Q2, ohc(2), "oh16", -1.0 / 32, OP.mult)
+        colop(Q3, ohc(3), "oh16", -1.0 / 32, OP.mult)
+        for t in range(RO - 1):
+            colop(W2 + t, ohc(1), "oh16", 2.0 * t, OP.mult)
+        act(T.jg[:], T.xf[:], "xf " + key(T2), "jg", AF.Identity, bias=col(T2), scale=16.0)
+        for h in range(16):
+            act(T.msk[:, h, :], T.xf[:, 0:16], "xf " + key(NPR), "msk%d" % h, AF.Relu, bias=col(NPR))
+        for h in range(2):
+            o = slice(8 * h, 8 * h + 8)
+            vts(T.dja[:, o], T.jg[:, 0:8], "jg", "dja%d" % h, float(W - 2560 - 1792), OP.add, 32.0, OP.mult)
+            vts(T.djb[:, o], T.jg[:, 0:8], "jg", "djb%d" % h, float(W - 2560), OP.add, -512.0, OP.mult)
         mat(M["n8k"], "n8k", PFC, -8192.0)
+        mat(M["nhf"], "nhf", PFC, -0.5)
         mat(T.tm1[:], "tm1", PP1, col(N15), key(N15))
         mat(T.tm2[:], "tm2", PFC, col(N15), key(N15))
         vtt(M["moh"], T.tm1[:], T.tm2[:], "tm1 tm2", "moh", OP.subtract)
         mat(M["mz0"], "mz0", PFC, ohc(0), "oh16")
         mat(T.tm1[:], "tm1", PP1, ohc(0), "oh16")
         vtt(M["mz1"], T.tm1[:], M["mz0"], "tm1 mz0", "mz1", OP.add)
-        vts(T.jg[:], T.xf[:], "xf " + key(T2), "jg", 16.0, OP.mult, col(T2), OP.add)
-        for h in range(2):
-            vts(T.dj[:, 8 * h:8 * h + 8], T.jg[:, 0:8], "jg", "dj%d" % h, float(W - 2560), OP.add)
-        for h in range(16):
-            vts(T.msk[:, h, :], T.xr[:, 0:16], "xr " + key(PRC), "msk%d" % h, col(PRC), OP.is_gt)
-        vset(T.inc[:, 0:8], 8191.0, "inc0")
-        vset(T.zer[:], 0.0, "zer")
-        for k in range(RO):
-            vset(T["rb%d" % k][:, CAP:CAP + 16], 0.0, "rbx%d" % k)
-        vset(T.pw[:, 0:CAP], 0.0, "pw")
-        vts(T.xi[:], T.iox[:, 0:128], "iox", "xi", 63, OP.bitwise_and)
-        vts(T.xs[:], T.iox[:, 0:128], "iox", "xs", 6, OP.arith_shift_right)
+        vts(T.xi[:], T.tm3[:], "tm3", "xi", 63, OP.bitwise_and)
+        vts(T.xs[:], T.tm3[:], "tm3", "xs", 6, OP.arith_shift_right)
         vts(T.tm1[:], T.xi[:], "xi oh16", "tm1", ohc(0), OP.mult)
         vts(T.tm2[:], T.xs[:], "xs oh16", "tm2", float(W0 // 64), OP.add, ohc(1), OP.mult)
         vtt(T.wdl[:], T.tm1[:], T.tm2[:], "tm1 tm2", "wdl", OP.add)
@@ -275,8 +289,6 @@ def rank_program(g, core, T, topo):
     HCUR = ["h0"]
     for X in XS:
         vcp(T.cl[:, CQ[X]], T.ca[:, CQ[X]], "ca" + X, "cl" + X)
-    vset(T.h0[:], 0.0, "h0")
-    vlist(0)
 
     def selmm(out, w, base, rhs, rk, start=True, stop=True):
         def f():
@@ -285,105 +297,122 @@ def rank_program(g, core, T, topo):
             return x
         op("t", f, base + " " + rk, w)
 
+    def every(n, X):
+        return " ".join(n + "b%d" % b for b in PIECES[X])
+
     def pieces(X):
         for i, b in enumerate(PIECES[X]):
             yield "b%d" % b, slice(512 * i, 512 * i + 512), slice(CQ[X].start + 32 * i, CQ[X].start + 32 * i + 32)
 
-    def do_step(t, s):
-        st = 2 * t + s
-        wn = W0 + B * t
-        old = CUR[0]
-        new = "cc" if old == "ca" else "ca"
+    TBANK = {"A": "b7", "B": "b6"}
+    CBANK = {"A": "b5", "B": "b6"}
+    CREG = {"A": T.b5[:, 0:96], "B": T.b6[:, 256:320]}
+    LBANK = {"A": "b7", "B": "b6"}
+    LREG = {"A": T.b7[:, 0:96], "B": T.b6[:, 320:384]}
+
+    def counts(t, s, X):
+        for bk, p, cq in pieces(X):
+            kw = T.kt[:, 0:W0 + B * t].indirect(T.cl[:, cq])
+            if t + s == 0:
+                vcp(T["kap" + X][:, p], kw, KT + " cl" + X, "kap" + bk)
+            else:
+                vtt(T["kap" + X][:, p], kw, T["ne" + X][:, p], KT + " cl" + X + " ne" + bk, "kap" + bk, OP.mult)
+
+    def total(X):
+        selmm(T[TBANK[X]][:, 0:NQ[X]], TBANK[X], "selt", T["kap" + X], every("kap", X))
+
+    def suffixes(t, X):
+        act(T["gg" + X][:], T.gt[:, 0:W0 + B * t].indirect(T.cl[:, CQ[X]]), GT + " cl" + X, "gg" + X, AF.Copy)
+
+    def targets(st, X):
+        c = CQ[X]
+        tk = TBANK[X]
+        tp = T[tk][:, 0:NQ[X]]
+        sc = slice(st * 160 + c.start, st * 160 + c.stop)
+        vts(T.pp[:, c], tp, tk, "pp" + X, 1.0 / 32, OP.mult, 0.25, OP.subtract)
+        vtt(T.vs[:, c], tp, T.v1[:, sc], tk + " v1_%d" % st, "vs" + X, OP.mult)
+        vtt(T.wp[:, c], T.pp[:, c], T.v31[:, sc], "pp" + X + " v31_%d" % st, "wp" + X, OP.mult)
+        vtt(T.vs[:, c], T.vs[:, c], T.wp[:, c], "vs" + X + " wp" + X, "vs" + X, OP.subtract)
+        vts(T.qq[:, c], T.vs[:, c], "vs" + X, "qq" + X, 1.0 / 256, OP.mult, 1024.0 - 127.5 / 256, OP.add)
+
+    def compare(X):
+        for bk, p, cq in pieces(X):
+            def f(bk=bk, p=p, cq=cq):
+                PE.matmul(T[bk][:], M["tri"], T["kap" + X][:, p], True, False)
+                for r in range(16):
+                    x = PE.matmul(T[bk][:, r::16], T.expa[:, 128 * r:128 * r + 128], T.qq[:, cq], False, r == 15)
+                return x
+            op("t", f, "tri kap" + bk + " qq" + X + " " + EXPA, bk)
+            act(T["cd" + X][:, p], T[bk][:], bk, "cd" + bk, AF.Sigmoid, bias=-16.0 * (32768 - 24), scale=-16.0)
+
+    def suffix_sum(X):
+        ap = T.b6[:, 64 + CQ[X].start:64 + CQ[X].stop]
+        selmm(ap, "b6", "selF", T["gg" + X], "gg" + X)
+        act(T.ff[:, CQ[X]], ap, "b6", "ff" + X, AF.Copy, bias=65536.0)
+
+    def first_sum(X):
+        selmm(CREG[X], CBANK[X], "selS", T["gg" + X], "gg" + X, True, False)
+
+    def pointer(t, X):
+        for bk, p, cq in pieces(X):
+            vtt(T["ds" + X][:, p], T.dtb[:, 0:W0 + B * t].indirect(T.cl[:, cq]), T["cd" + X][:, p], DT + " cl" + X + " cd" + bk, "ds" + bk, OP.mult)
+
+    def pointer_sum(X):
+        selmm(CREG[X], CBANK[X], "seld", T["ds" + X], every("ds", X), False, True)
+
+    def context(s, X, new):
+        c = CQ[X]
+        vtt(T.mm[:, c], CREG[X], T.ff[:, c], CBANK[X] + " ff" + X, "mm" + X, OP.min)
+        if X == "A":
+            vts(T.e8[:], T.b5[:, 0:8], "b5", "e8", 70000.0, OP.is_gt)
+        if s == 1:
+            vts(T.es[:, c], CREG[X], CBANK[X], "es" + X, 70000.0, OP.is_gt)
+        vts(T[new][:, c], T.mm[:, c], "mm" + X, new + X, 4095, OP.bitwise_and)
+        vcp(T.cl[:, c], T[new][:, c], new + X, "cl" + X)
+
+    def mark_piece(s, X, bk, p):
+        mms(T[bk][:], [(M["i14"], T["kap" + X][:, p]), (M["e15"], T["ds" + X][:, p])], "i14 e15 kap" + bk + " ds" + bk, bk)
+        if s == 0:
+            act(T["ne" + X][:, p], T[bk][:], bk, "ne" + bk, AF.Sigmoid, bias=256.0 * (2.0 ** 23 - 0.5), scale=-256.0)
+        else:
+            act(T["em" + X][:, p], T[bk][:], bk, "em" + bk, AF.Sign, bias=-(2.0 ** 23 - 0.5))
+
+    def slots(X):
+        c = CQ[X]
+        ik = "inc0" if X == "A" else "incA"
+        mms(T.b7[:, c], [(M["tri"], T.es[:, c]), (M["n8k"], T.es[:, c])], "tri n8k es" + X, "b7")
+        mms(T.b6[:, 0:NQ[X]], [(M["blk"], T.es[:, c])], "blk es" + X, "b6")
+        op("v", lambda: V.tensor_tensor_scan(T.inc[:, 8 + c.start:8 + c.stop], T.b6[:, 0:NQ[X]], T.zer[:, 0:NQ[X]], T.inc[:, 7 + c.start:8 + c.start], OP.add, OP.add), "b6 zer " + ik, "inc" + X)
+        vtt(T.sa[:, c], T.inc[:, 7 + c.start:7 + c.stop], T.b7[:, c], "b7 inc" + X + " " + ik, "sa" + X, OP.add)
+        vtt(T.sb2[:, c], T.sa[:, c], T.jg[:, c], "jg sa" + X, "sb" + X, OP.min)
+        vcp(T.sl[:, c], T.sb2[:, c], "sb" + X, "sl" + X)
+        vts(T.rl[:, c], T.sa[:, c], "sa" + X, "rl" + X, float(CAP), OP.min)
+
+    def first_escape(old):
         hold = HCUR[0]
         hnew = "h1" if hold == "h0" else "h0"
-        tbank = {"A": "b7", "B": "b6"}
-        for X in XS:
-            kw = T.kt[:, 0:wn].indirect(T.cl[:, CQ[X]])
-            if st == 0:
-                vcp(T["kap" + X][:], kw, KT + " cl" + X, "kap" + X)
-            else:
-                vtt(T["kap" + X][:], kw, T["ne" + X][:], KT + " cl" + X + " ne" + X, "kap" + X, OP.mult)
-        if st == 0:
-            late_constants()
-        for X in XS:
-            act(T["gg" + X][:], T.gt[:, 0:wn].indirect(T.cl[:, CQ[X]]), GT + " cl" + X, "gg" + X, AF.Copy)
-        for X in XS:
-            c = CQ[X]
-            tk = tbank[X]
-            tp = T[tk][:, 0:NQ[X]]
-            selmm(tp, tk, "selt", T["kap" + X], "kap" + X)
-            vts(T.pp[:, c], tp, tk, "pp" + X, 1.0 / 32, OP.mult, 0.25, OP.subtract)
-            sc = slice(st * 160 + c.start, st * 160 + c.stop)
-            vtt(T.vs[:, c], tp, T.v1[:, sc], tk + " v1_%d" % st, "vs" + X, OP.mult)
-            vtt(T.wp[:, c], T.pp[:, c], T.v31[:, sc], "pp" + X + " v31_%d" % st, "wp" + X, OP.mult)
-            vtt(T.vs[:, c], T.vs[:, c], T.wp[:, c], "vs" + X + " wp" + X, "vs" + X, OP.subtract)
-            vts(T.qq[:, c], T.vs[:, c], "vs" + X, "qq" + X, 1.0 / 256, OP.mult, 1024.0 - 127.5 / 256, OP.add)
-        for X in XS:
-            for bk, p, cq in pieces(X):
-                def f(bk=bk, p=p, cq=cq, X=X):
-                    PE.matmul(T[bk][:], M["tri"], T["kap" + X][:, p], True, False)
-                    for r in range(16):
-                        x = PE.matmul(T[bk][:, r::16], T.expa[:, 128 * r:128 * r + 128], T.qq[:, cq], False, r == 15)
-                    return x
-                op("t", f, "tri kap" + X + " qq" + X + " " + EXPA, bk)
-                act(T["cd" + X][:, p], T[bk][:], bk, "cd" + X, AF.Sigmoid, bias=-16.0 * (32768 - 24), scale=-16.0)
-            if X == "A":
-                for Z in XS:
-                    selmm(T.b6[:, 64 + CQ[Z].start:64 + CQ[Z].stop], "b6", "selF", T["gg" + Z], "gg" + Z)
-                act(T.ff[:], T.b6[:, 64:224], "b6", "ff", AF.Copy, bias=65536.0)
-        for X in XS:
-            vtt(T["ds" + X][:], T.dtb[:, 0:wn].indirect(T.cl[:, CQ[X]]), T["cd" + X][:], DT + " cl" + X + " cd" + X, "ds" + X, OP.mult)
-        for X in XS:
-            c = CQ[X]
-            ap = T.b5[:, 0:NQ[X]]
-            selmm(ap, "b5", "selS", T["gg" + X], "gg" + X, True, False)
-            selmm(ap, "b5", "seld", T["ds" + X], "ds" + X, False, True)
-            vtt(T.mm[:, c], ap, T.ff[:, c], "b5 ff", "mm" + X, OP.min)
-            if X == "A":
-                vts(T.e8[:], T.b5[:, 0:8], "b5", "e8", 70000.0, OP.is_gt)
-            if s == 1:
-                vts(T.es[:, c], ap, "b5", "es" + X, 70000.0, OP.is_gt)
-            vts(T[new][:, c], T.mm[:, c], "mm" + X, new + X, 4095, OP.bitwise_and)
-            vcp(T.cl[:, c], T[new][:, c], new + X, "cl" + X)
-            if s == 1:
-                act(T["gg" + X][:], T.lt[:, 0:wn].indirect(T.cl[:, c]), LT + " cl" + X, "gg" + X, AF.Copy)
-                mms(T.b7[:, c], [(M["tri"], T.es[:, c]), (M["n8k"], T.es[:, c])], "tri n8k es" + X, "b7")
-                mms(T.b6[:, 0:NQ[X]], [(M["blk"], T.es[:, c])], "blk es" + X, "b6")
-            if s == 0 or t < RO - 1:
-                for bk, p, cq in pieces(X):
-                    mms(T[bk][:], [(M["i14"], T["kap" + X][:, p]), (M["e15"], T["ds" + X][:, p])], "i14 e15 kap" + X + " ds" + X, bk)
-                    if s == 0:
-                        act(T["ne" + X][:, p], T[bk][:], bk, "ne" + X, AF.Sigmoid, bias=256.0 * (2.0 ** 23 - 0.5), scale=-256.0)
-                    else:
-                        act(T["em" + X][:, p], T[bk][:], bk, "em" + X, AF.Sign, bias=-(2.0 ** 23 - 0.5))
-            if s == 1:
-                o = c.start
-                ik = "inc0" if X == "A" else "incA"
-                op("v", lambda: V.tensor_tensor_scan(T.inc[:, 8 + c.start:8 + c.stop], T.b6[:, 0:NQ[X]], T.zer[:, 0:NQ[X]], T.inc[:, 7 + o:8 + o], OP.add, OP.add), "b6 zer " + ik, "inc" + X)
-                vtt(T.sa[:, c], T.inc[:, 7 + c.start:7 + c.stop], T.b7[:, c], "b7 inc" + X + " " + ik, "sa" + X, OP.add)
-                vtt(T.sb2[:, c], T.sa[:, c], T.jg[:, c], "jg sa" + X, "sb" + X, OP.min)
-                vcp(T.sl[:, c], T.sb2[:, c], "sb" + X, "sl" + X)
-                vts(T.rl[:, c], T.sa[:, c], "sa" + X, "rl" + X, float(CAP), OP.min)
-        if st + 1 < RO * SP:
-            vlist(st + 1)
-        if s == 1:
-            send(t)
         vts(T.ht[:], T[hold][:], hold, "ht", 0.0, OP.is_equal)
-        vts(T.hu[:], T[old][:, 0:8], old + "A", "hu", 1.0, OP.add)
-        vtt(T.ht[:], T.ht[:], T.hu[:], "ht hu", "ht", OP.mult)
+        vtt(T.ht[:], T.ht[:], T[old][:, 0:8], "ht " + old + "A", "ht", OP.mult)
         vtt(T.ht[:], T.ht[:], T[hold][:], "ht " + hold, "ht", OP.add)
         vtt(T[hnew][:], T.ht[:], T.e8[:], "ht e8", hnew, OP.mult)
-        CUR[0] = new
         HCUR[0] = hnew
-        return old, hold
+
+    def flip():
+        old = CUR[0]
+        CUR[0] = "cc" if old == "ca" else "ca"
+        return old, CUR[0]
 
     def send(t):
+        if t < RO - 1:
+            vlist(SP * t + 2)
+            vlist(SP * t + 3)
         for X in XS:
-            pwi = T.pw[:].indirect(T.sl[:, CQ[X]])
-            if t < RO - 1:
-                vtt(pwi, T["gg" + X][:], T["em" + X][:], "sl" + X + " gg" + X + " em" + X, "pw", OP.mult)
-            else:
-                vcp(pwi, T["gg" + X][:], "sl" + X + " gg" + X, "pw")
+            for bk, p, cq in pieces(X):
+                pwi = T.pw[:].indirect(T.sl[:, cq])
+                if t < RO - 1:
+                    vtt(pwi, T["gg" + X][:, p], T["em" + X][:, p], "sl" + X + " lg" + bk + " em" + bk, "pw", OP.mult)
+                else:
+                    vcp(pwi, T["gg" + X][:, p], "sl" + X + " lg" + bk, "pw")
         deps("g", ["pw"], [])
         dst = T.cores[(rank + 1) % len(T.cores)]
         src = T.cores[(rank - 1) % len(T.cores)]
@@ -393,33 +422,46 @@ def rank_program(g, core, T, topo):
         cnt["arr%d" % t] = len(topo.engines(src, core))
         mark(("rem", "snt%d" % t, cnt["snt%d" % t]), ["pw"], [])
         lw["rb%d" % t] = ("rem", "arr%d" % t, cnt["arr%d" % t])
+        if t < RO - 1:
+            fill(T.pw[:, 0:CAP], [[0, CAP]], 0, "pw")
+
+    PEND = []
 
     def hop_recv(t):
-        cur = CUR[0]
-        new = "cc" if cur == "ca" else "ca"
+        old, new = flip()
+        PEND[:] = [old, new]
         RB = "rb%d rbx%d" % (t, t)
         win = T["rb%d" % t][:, 0:CAP + 16]
         for X in XS:
-            act(T["gg" + X][:], win.indirect(T.rl[:, CQ[X]]), RB + " rl" + X, "gg" + X, AF.Abs)
-        if t < RO - 1:
-            for X in XS:
-                vtt(T["ne" + X][:], win.indirect(T.rl[:, CQ[X]]), T["em" + X][:], RB + " rl" + X + " em" + X, "ne" + X, OP.is_gt)
-        for X in XS:
-            c = CQ[X]
-            bp = T.b6[:, 0:NQ[X]]
-            selmm(bp, "b6", "selS", T["gg" + X], "gg" + X)
-            vts(T.nr[:, c], bp, "b6", "nr" + X, 1.0, OP.is_lt)
-            vts(T.rc[:, c], bp, "b6", "rc" + X, 130.0, OP.subtract, 0.0, OP.max)
-            vtt(T.c1[:, c], T[cur][:, c], T.nr[:, c], cur + X + " nr" + X, "c1" + X, OP.mult)
-            if t < RO - 1:
-                vtt(T[new][:, c], T.c1[:, c], T.rc[:, c], "c1" + X + " rc" + X, new + X, OP.add)
-                vcp(T.cl[:, c], T[new][:, c], new + X, "cl" + X)
-            else:
-                vtt(T.yo[:, c], T.c1[:, c], T.rc[:, c], "c1" + X + " rc" + X, "yo" + X, OP.add)
-        h = HCUR[0]
-        if t < RO - 1:
+            ggk = "gg" + X + " " + every("lg", X)
+            if t == RO - 1:
+                act(T["gg" + X][:], win.indirect(T.rl[:, CQ[X]]), RB + " rl" + X, ggk, AF.Abs)
+                selmm(LREG[X], LBANK[X], "selS", T["gg" + X], "gg" + X)
+                continue
+            act(T["cd" + X][:], win.indirect(T.rl[:, CQ[X]]), RB + " rl" + X, every("cd", X), AF.Copy)
+            act(T["gg" + X][:], T["cd" + X][:], every("cd", X), ggk, AF.Abs)
+            selmm(LREG[X], LBANK[X], "selS", T["gg" + X], "gg" + X)
+            for bk, p, cq in pieces(X):
+                mms(T[bk][:], [(M["idb"], T["cd" + X][:, p]), (M["nhf"], T["em" + X][:, p])], "idb nhf cd" + bk + " em" + bk, bk)
+                act(T["ne" + X][:, p], T[bk][:], bk, "ne" + bk, AF.Sigmoid, scale=256.0)
+        link_context(t, "A")
+        if t == RO - 1:
+            link_context(t, "B")
+        else:
+            h = HCUR[0]
             vtt(T[h][:], T[h][:], T.nr[:, 0:8], h + " nrA", h, OP.mult)
-        CUR[0] = new
+
+    def link_context(t, X):
+        old, new = PEND
+        c = CQ[X]
+        vts(T.nr[:, c], LREG[X], LBANK[X], "nr" + X, 1.0, OP.is_lt)
+        vts(T.rc[:, c], LREG[X], LBANK[X], "rc" + X, 130.0, OP.subtract, 0.0, OP.max)
+        vtt(T.c1[:, c], T[old][:, c], T.nr[:, c], old + X + " nr" + X, "c1" + X, OP.mult)
+        if t < RO - 1:
+            vtt(T[new][:, c], T.c1[:, c], T.rc[:, c], "c1" + X + " rc" + X, new + X, OP.add)
+            vcp(T.cl[:, c], T[new][:, c], new + X, "cl" + X)
+        else:
+            vtt(T.yo[:, c], T.c1[:, c], T.rc[:, c], "c1" + X + " rc" + X, "yo" + X, OP.add)
 
     def write_back(t, old, hb):
         full = t < RO - 1
@@ -428,28 +470,36 @@ def rank_program(g, core, T, topo):
         wsl = slice(wn, wn + B)
         l8 = T.cl[:, 0:8]
         lf = T.fdu[:, 0:8]
-        vts(T.cnd[:], T[hb][:], hb, "cnd", 0.0, OP.is_gt)
-        vts(T.ht[:], T.e8[:], "e8", "ht", -1.0, OP.mult, 1.0, OP.add)
-        vtt(T.cnd[:], T.cnd[:], T.ht[:], "cnd ht", "cnd", OP.mult)
-        vts(T.ka[:, 0:8], T[hb][:], hb, "ka0", 3841.0, OP.subtract)
+        vts(T.cnd[:], T.e8[:], "e8", "cnd", 8192.0, OP.mult)
+        vtt(T.cnd[:], T[hb][:], T.cnd[:], hb + " cnd", "cnd", OP.is_gt)
+        vts(T.ka[:, 0:8], T[hb][:], hb, "ka0", 3840.0, OP.subtract)
         vts(T.ka[:, 8:16], T[old][:, 0:8], old + "A", "ka1", 3840.0, OP.subtract)
-        vts(T.ka[:, 16:24], T[cur][:, 0:8], cur + "A", "ka2", 3840.0, OP.subtract)
-        vts(T.fd[:], T.ka[:, 0:16], "ka0 ka1", "fd", 3840.0, OP.add, 0.0, OP.max)
-        vcp(T.fdu[:], T.fd[:], "fd", "fdu")
+        vts(T.fdu[:], T.ka[:], "ka0 ka1", "fdu", 3840.0, OP.add)
         vtt(T.ka[:, 0:8], T.ka[:, 0:8], T.cnd[:], "ka0 cnd", "ka0", OP.mult)
         vtt(T.ka[:, 8:16], T.ka[:, 8:16], T.cnd[:], "ka1 cnd", "ka1", OP.mult)
-        vts(T.k16[:], T.ka[:], "ka0 ka1 ka2", "k16", 2048.0, OP.add)
-        vts(T.k32[:], T.ka[:], "ka0 ka1 ka2", "k32", 2048.0, OP.add, -32.0, OP.mult)
+        vts(T.k16[:, 0:16], T.ka[:], "ka0 ka1", "k16a", 2048.0, OP.add)
+        vts(T.k32[:], T.ka[:], "ka0 ka1", "k32", 2048.0, OP.add, -32.0, OP.mult)
+        nk = 16
+        if full:
+            nk = 32
+            vts(T.dgi[:, 0:8], T[cur][:, 0:8], cur + "A", "dgi0", 63, OP.bitwise_and)
+            vts(T.dgi[:, 8:16], T[cur][:, 0:8], cur + "A", "dgi1", 6, OP.arith_shift_right)
+            vcp(T.k16[:, 16:32], T.dgi[:], "dgi0 dgi1", "k16b")
 
         def frow():
             for r in range(16):
-                x = PE.matmul(T.b4[:, r:384:16], T.expa[:, 128 * r:128 * r + 128], T.k16[:], True, True)
+                x = PE.matmul(T.b7[:, r:16 * nk:16], T.expa[:, 128 * r:128 * r + 128], T.k16[:, 0:nk], True, True)
             return x
-        op("t", frow, EXPA + " k16", "b4")
-        mms(T.b5[:, 0:B], [(M["moh"], T.cdA[:, 0:B]), (M["mz0"], T.ones[:, 0:B])], "moh cdA mz0 ones", "b5")
+        op("t", frow, EXPA + " k16a k16b", "b7")
+        mms(T.b5[:, 0:B], [(M["moh"], T.cdA[:, 0:B]), (M["mz0"], T.ones[:, 0:B])], "moh cdb0 mz0 ones", "b5")
         act(T.ohf[:], T.b5[:, 0:B], "b5", "ohf", AF.Copy)
         act(T.oh3[:], T.b5[:, 0:B], "b5", "oh3", AF.Copy, scale=32.0)
+        act(T.o33[:], T.b5[:, 0:B], "b5", "o33", AF.Copy, bias=-EPS, scale=33.0 + EPS)
+        act(T.kf[:], T.kt[:, 0:wn].indirect(lf), KT + " fdu", "kf", AF.Copy)
+        act(T.k2[:], T.kf[:], "kf", "k2", AF.Copy, bias=33.0, scale=-1.0)
         if full:
+            act(T.xv[:], T.xf[:, 0:B], "xf", "xv", AF.Copy, bias=float(wn))
+            act(T.wv[:], T.wdl[:], "wdl " + key(W2 + t), "wv", AF.Identity, bias=col(W2 + t))
             act(T.ohb[:], T.b5[:, 0:B], "b5", "ohb", AF.Copy)
             act(T.g1[:], T.gt[:, 0:wn].indirect(l8), GT + " clA " + key(R01), "g1", AF.Copy, scale=col(R01))
             act(T.gf[:], T.gt[:, 0:wn].indirect(lf), GT + " fdu", "gf", AF.Copy)
@@ -457,10 +507,13 @@ def rank_program(g, core, T, topo):
         for k in range(2):
             for p in range(8):
                 i = 8 * k + p
-                vts(T.eq[:, i, 0:B - 16 * p], T.b4[:, B * k + 16 * p:B * k + B], "b4 k32", "eq%d" % i, T.k32[:, i:i + 1], OP.is_equal)
+                vts(T.eq[:, i, 0:B - 16 * p], T.b7[:, B * k + 16 * p:B * k + B], "b7 k32", "eq%d" % i, T.k32[:, i:i + 1], OP.is_equal)
         eqs = " ".join("eq%d" % i for i in range(16))
         vtt(T.eq[:, :, 0:16], T.eq[:, :, 0:16], T.msk[:, :, :], eqs + " " + " ".join("msk%d" % h for h in range(16)), eqs, OP.mult)
-        vts(T.cr[:], T.b4[:, 0:256], "b4", "cr", -65536.0, OP.is_gt)
+        vts(T.cr[:], T.b7[:, 0:256], "b7", "cr", -65536.0, OP.is_gt, 1.0, OP.subtract)
+        if full:
+            act(T.xt[:], T.b7[:, 256:384], "b7 " + key(Q2), "xt", AF.Copy, scale=col(Q2))
+            act(T.xw[:], T.b7[:, 384:512], "b7 " + key(Q3), "xw", AF.Copy, scale=col(Q3))
 
         def fc():
             for k in range(2):
@@ -468,23 +521,18 @@ def rank_program(g, core, T, topo):
                     x = PE.matmul(T.b6[:, B * k + 16 * p:B * k + B], M["blk"], T.eq[:, 8 * k + p, 0:B - 16 * p], p == 0, p == 7)
             return x
         op("t", fc, "blk " + eqs, "b6")
-        djk = " dj0 dj1"
+        dj = " dja0 dja1 djb0 djb1"
         vts(T.chi[:], T.kt[:, 0:wn].indirect(l8), KT + " clA", "chi", 1.0 / 64, OP.mult, 0.25, OP.add)
-        vcp(T.kf[:], T.kt[:, 0:wn].indirect(lf), KT + " fdu", "kf")
-        vtt(T.fy[:], T.fd[:], T.dj[:], "fd" + djk, "fy", OP.subtract)
-        vts(T.fy[:], T.fy[:], "fy", "fy", 1.0 / 16, OP.mult)
-        vts(T.kr[:], T.b6[:, 0:256], "b6", "kr", 0.0, OP.is_equal)
-        vtt(T.kr[:], T.kr[:], T.cr[:], "kr cr", "kr", OP.mult)
-        selmm(T.b7[:, 0:16], "b7", "selt", T.kr, "kr")
+        vtt(T.fy[:], T.k32[:], T.dja[:], "k32" + dj, "fy", OP.add)
+        vtt(T.k2[:], T.k2[:], T.ohf[:], "k2 ohf", "k2", OP.mult)
+        vtt(T.kr[:], T.b6[:, 0:256], T.cr[:], "b6 cr", "kr", OP.is_le)
+        selmm(T.b5[:, 128:144], "b5", "selt", T.kr, "kr")
         vtt(T.chf[:], T.chi[:], T.kr[:, 0:B], "chi kr", "chf", OP.mult)
         vts(T.cm[:], T.chf[:], "chf", "cm", 1.0, OP.min, 1.0 + EPS, OP.mult)
         vts(T.chf[:], T.chf[:], "chf", "chf", 32.0, OP.mult, EPS, OP.subtract)
-        vts(T.k2[:], T.kf[:], "kf", "k2", -1.0, OP.mult, 33.0, OP.add)
-        vtt(T.k2[:], T.k2[:], T.ohf[:], "k2 ohf", "k2", OP.mult)
-        vts(T.o33[:], T.ohf[:], "ohf", "o33", 33.0 + EPS, OP.mult, EPS, OP.subtract)
-        vtt(T.fy[:], T.b7[:, 0:16], T.fy[:], "b7 fy", "fy", OP.mult)
-        vtt(T.fy[:], T.fy[:], T.dj[:], "fy" + djk, "fy", OP.add)
-        vcp(T.lw[:], T.fy[:], "fy", "lw")
+        vtt(T.fy[:], T.b5[:, 128:144], T.fy[:], "b5 fy", "fy", OP.mult)
+        vtt(T.fy[:], T.fy[:], T.djb[:], "fy" + dj, "fy", OP.add)
+        vts(T.lw[:], T.fy[:], "fy", "lw", -1.0 / 512, OP.mult)
         vtt(T.kt[:, wsl], T.chf[:], T.cm[:], "chf cm", KT, OP.add)
         vtt(T.kt[:].indirect(T.lw[:, 0:8]), T.kf[:], T.k2[:], "kf k2 lw", KT, OP.add)
         if full:
@@ -492,13 +540,12 @@ def rank_program(g, core, T, topo):
             vcp(T.tb[:, wsl], T.tb[:, 0:wn].indirect(l8), TB + " clA", TB)
             vts(T.dtb[:, wsl], T.dtb[:, 0:wn].indirect(l8), DT + " clA " + key(D15), DT, col(D15), OP.max)
             vts(T.xi[:], T.xi[:], "xi", "xi", 4, OP.arith_shift_right)
-            vts(T.xw[:], T.xf[:, 0:B], "xf", "xw", float(wn), OP.add)
-            vtt(T.xw[:], T.xw[:], T.xi[:], "xw xi", "xw", OP.subtract)
-            vtt(T.xw[:], T.xw[:], T.ohf[:], "xw ohf", "xw", OP.mult)
-            vtt(T.xw[:], T.xw[:], T.xi[:], "xw xi", "xw", OP.add)
-            vts(T.s16[:, 0:B], T.xw[:], "xw", "s16", 1792.0, OP.subtract)
+            vtt(T.xv[:], T.xv[:], T.xi[:], "xv xi", "xv", OP.subtract)
+            vtt(T.xv[:], T.xv[:], T.ohf[:], "xv ohf", "xv", OP.mult)
+            vtt(T.xv[:], T.xv[:], T.xi[:], "xv xi", "xv", OP.add)
+            vts(T.s16[:, 0:B], T.xv[:], "xv", "s16", 1792.0, OP.subtract)
             mms(T.b5[:, 0:B], [(M["mdf"], T.s16[:, 0:B]), (M["mfl"], T.ones[:, 0:B])], "mdf mfl s16 ones", "b5")
-            vts(T.xs[:], T.xw[:], "xw", "xs", 16.0, OP.mult)
+            vts(T.xs[:], T.xv[:], "xv", "xs", 16.0, OP.mult)
             vcp(T.tb[:].indirect(T.lw[:, 0:8]), T.xs[:], "xs lw", TB)
         vtt(T.k2[:], T.kt[:, 0:wn].indirect(T.fdu[:, 8:16]), T.oh3[:], KT + " fdu oh3", "k2", OP.add)
         vts(T.k2[:], T.k2[:], "k2", "k2", 481.0, OP.min)
@@ -506,26 +553,78 @@ def rank_program(g, core, T, topo):
         if not full:
             return
         vcp(T.rr[:, 0:B], T.b5[:, 0:B], "b5", "rr0")
-        vtt(T.xt[:], T.b5[:, 0:B], T.rr[:, 0:B], "b5 rr0", "xt", OP.subtract)
-        vcp(T.dtb[:].indirect(T.lw[:, 0:8]), T.xt[:], "xt lw", DT)
+        vtt(T.xd[:], T.b5[:, 0:B], T.rr[:, 0:B], "b5 rr0", "xd", OP.subtract)
+        vcp(T.dtb[:].indirect(T.lw[:, 0:8]), T.xd[:], "xd lw", DT)
         mms(T.b6[:, 0:B], [(M["mz1"], T.ohb[:])], "mz1 ohb", "b6")
-        vts(T.rci[:], T.b4[:, 256:384], "b4", "rci", -1.0 / 32, OP.mult, 1792.0, OP.add)
-        vts(T.xi[:], T.rci[:], "rci", "xi", 63, OP.bitwise_and)
-        vts(T.xs[:], T.rci[:], "rci", "xs", 6, OP.arith_shift_right)
-        vts(T.xt[:], T.xi[:], "xi oh16", "xt", ohc(2), OP.mult)
-        vts(T.xw[:], T.xs[:], "xs oh16", "xw", ohc(3), OP.mult)
         vtt(T.xt[:], T.xt[:], T.xw[:], "xt xw", "xt", OP.add)
         vtt(T.gt[:, wsl], T.xt[:], T.g1[:], "xt g1", GT, OP.add)
-        vts(T.xw[:], T.ones[:, 0:B], "ones oh16", "xw", 2.0 * t, OP.mult, ohc(1), OP.mult)
-        vtt(T.xw[:], T.xw[:], T.wdl[:], "xw wdl", "xw", OP.add)
-        vtt(T.xw[:], T.xw[:], T.gf[:], "xw gf", "xw", OP.subtract)
-        vtt(T.g1[:], T.b6[:, 0:B], T.xw[:], "b6 xw", "g1", OP.mult)
-        vtt(T.gt[:].indirect(T.lw[:, 0:8]), T.gf[:], T.g1[:], "gf g1 lw", GT, OP.add)
-        vset(T.pw[:, 0:CAP], 0.0, "pw")
+        vtt(T.wv[:], T.wv[:], T.gf[:], "wv gf", "wv", OP.subtract)
+        vtt(T.g2[:], T.b6[:, 0:B], T.wv[:], "b6 wv", "g2", OP.mult)
+        vtt(T.gt[:].indirect(T.lw[:, 0:8]), T.gf[:], T.g2[:], "gf g2 lw", GT, OP.add)
 
     for t in range(RO):
-        do_step(t, 0)
-        old, hb = do_step(t, 1)
+        for s in range(SP):
+            st = SP * t + s
+            if s == 0:
+                if t == 0:
+                    digits()
+                    pointers(0)
+                    vlist(0)
+                    vlist(1)
+                counts(t, 0, "A")
+                total("A")
+                if t > 0:
+                    suffixes(t, "A")
+                    link_context(t - 1, "B")
+                else:
+                    pointers(1)
+                    suffixes(t, "A")
+            targets(st, "A")
+            compare("A")
+            counts(t, s, "B")
+            total("B")
+            targets(st, "B")
+            if st == 0:
+                pointers(2)
+            if s == 1:
+                first_escape(old)
+                hb = HCUR[0]
+            compare("B")
+            suffix_sum("A")
+            first_sum("A")
+            suffixes(t, "B")
+            if st == 0:
+                late_constants()
+            pointer(t, "A")
+            pointer(t, "B")
+            old, new = flip()
+            pointer_sum("A")
+            context(s, "A", new)
+            if s == 0:
+                for bk, p, cq in pieces("A"):
+                    mark_piece(0, "A", bk, p)
+            suffix_sum("B")
+            first_sum("B")
+            pointer_sum("B")
+            if s == 0:
+                for bk, p, cq in pieces("B"):
+                    mark_piece(0, "B", bk, p)
+                counts(t, 1, "A")
+                context(0, "B", new)
+                total("A")
+                suffixes(t, "A")
+                continue
+            for X in XS:
+                if X == "B":
+                    context(1, "B", new)
+                slots(X)
+                for bk, p, cq in pieces(X):
+                    act(T["gg" + X][:, p], T.lt[:, 0:W0 + B * t].indirect(T.cl[:, cq]), LT + " cl" + X, "gg" + X + " lg" + bk, AF.Copy)
+                    if t < RO - 1:
+                        mark_piece(1, X, bk, p)
+        send(t)
+        if t < RO - 1:
+            first_escape(old)
         write_back(t, old, hb)
         if t == RO - 1:
             for h in range(2):

from concourse.mybir import dt, AluOpType as OP, ActivationFunctionType as AF

EPS = 2.0 ** -14
W0, B, LN, RO, SP, CAP = 3072, 128, 2560, 4, 2, 768
W = W0 + RO * B
WD = W + B
XS = "AB"
CQ = {"A": slice(0, 96), "B": slice(96, 160)}
NQ = {"A": 96, "B": 64}
PIECES = {"A": [0, 1, 2], "B": [3, 4]}

_F, _H, _I, _B, _U = "float32", "float16", "int32", "bfloat16", "uint16"
SCRATCH = {}
for _n, _w, _d in (
        ("tb", WD, _I), ("kt", WD, _F), ("dtb", WD, _F), ("gt", WD, _B), ("lt", WD, _B),
        ("ci", 1024, _I), ("cb", 1024, _B), ("sg", 1024, _B), ("cb2", 1024, _B), ("sg2", 1024, _B), ("si", 1024, _I), ("s16", 1024, _H), ("rr", 1024, _I),
        ("dn", 576, _I), ("dg", 1152, _I), ("dgb", 1152, _B), ("v1", 1280, _F), ("v31", 1280, _F),
        ("iop", 1, _I), ("pi", 2, _I), ("xf", 160, _F), ("xg", 128, _F), ("xr", 128, _F),
        ("pc", 32, _F), ("oh16", 16, _F), ("m32", 16, _F), ("jg", 160, _F), ("dja", 16, _F), ("djb", 16, _F),
        ("mats", 14 * 128, _B), ("sels", 5 * 160, _B), ("expa", 2048, _B), ("ones", 512, _B), ("tm1", 128, _F), ("tm2", 128, _F), ("tm3", 128, _I),
        ("ca", 160, _I), ("cc", 160, _I), ("cl", 160, _U), ("pp", 160, _I), ("vs", 160, _F), ("wp", 160, _F), ("qq", 160, _H),
        ("ff", 160, _F), ("mm", 160, _I), ("es", 160, _B), ("inc", 168, _F), ("zer", 96, _F), ("sa", 160, _F), ("sb2", 160, _F),
        ("sl", 160, _U), ("rl", 160, _U), ("nr", 160, _F), ("c1", 160, _F), ("rc", 160, _F), ("yo", 160, _F), ("pw", 2 * LN, _B),
        ("h0", 8, _F), ("h1", 8, _F), ("ht", 8, _F), ("e8", 8, _F), ("cnd", 8, _F), ("dgi", 16, _I),
        ("ka", 16, _F), ("k32", 16, _F), ("k16", 32, _H), ("fdu", 16, _U), ("fy", 16, _F), ("lw", 16, _U),
        ("kr", 256, _B), ("cr", 256, _F), ("ohb", 128, _B), ("ohf", 128, _F), ("oh3", 128, _F), ("o33", 128, _F),
        ("chi", 128, _I), ("chf", 128, _F), ("cm", 128, _F), ("kf", 128, _F), ("k2", 128, _F), ("xi", 128, _I), ("xs", 128, _I),
        ("xt", 128, _F), ("xw", 128, _F), ("xv", 128, _F), ("xd", 128, _F), ("wv", 128, _F), ("g1", 128, _B), ("g2", 128, _B), ("gf", 128, _B),
        ("wdl", 128, _F), ("ynb", W, _B)):
    SCRATCH[_n] = ("sbuf", [128, _w], _d)
SCRATCH["vr"] = ("sbuf", [8, 20480], _B)
SCRATCH["eq"] = ("sbuf", [128, 16, 128], _B)
SCRATCH["msk"] = ("sbuf", [128, 16, 16], _B)
for _x in XS:
    for _n, _d in (("kap", _H), ("ds", _H), ("gg", _B), ("ne", _B), ("em", _B), ("cd", _B)):
        SCRATCH[_n + _x] = ("sbuf", [128, 16 * NQ[_x]], _d)
for _k in range(RO):
    SCRATCH["rb%d" % _k] = ("sbuf", [128, CAP + 16], _B)
for _k in range(8):
    SCRATCH["b%d" % _k] = ("psum", [128, 512], _F)
SEMAPHORES = ["cv", "ct", "cs", "cg"] + ["ld%d" % k for k in range(16)] + ["gd%d" % k for k in range(6)] + ["arr%d" % k for k in range(RO)] + ["snt%d" % k for k in range(RO)]


def rank_program(g, core, T, topo):
    rank = T.rank_of(core)
    if rank is None:
        return
    E = {"v": g.vector, "t": g.tensor, "s": g.scalar, "g": g, "y": g.sync}
    V, S, PE = g.vector, g.scalar, g.tensor
    cnt, waited, lw, lr = {}, {}, {}, {}

    def need(eng, sem, val):
        if waited.get((eng, sem), 0) < val:
            E[eng].wait_ge(T.sem[sem], val)
            waited[(eng, sem)] = val

    def deps(eng, r, w):
        todo = {}
        ds = [lw[k] for k in list(r) + list(w) if k in lw]
        for k in w:
            ds += list(lr.get(k, {}).values())
        for d in ds:
            if not (d[0] == eng == "t"):
                todo[d[1]] = max(todo.get(d[1], 0), d[2])
        for s in todo:
            need(eng, s, todo[s])

    def mark(d, r, w):
        for k in w:
            lw[k] = d
            lr[k] = {}
        for k in r:
            if k not in w:
                lr.setdefault(k, {})[d[1]] = d

    def op(eng, fn, r="", w=""):
        r = r.split()
        w = w.split()
        w = w + [k for k in r if len(k) == 2 and k[0] == "b" and k not in w]
        deps(eng, r, w)
        sem = "c" + eng
        cnt[sem] = cnt.get(sem, 0) + 1
        fn().then_inc(T.sem[sem], 1)
        mark((eng, sem, cnt[sem]), r, w)

    def dma(eng, out, in_, sem, r="", w=""):
        r = r.split()
        w = w.split()
        deps(eng, r, w)
        cnt[sem] = cnt.get(sem, 0) + 16
        E[eng].dma_start(out, in_).then_inc(T.sem[sem], 16)
        mark(("dma", sem, cnt[sem]), r, w)

    def vts(out, in0, r, w, s1, o0, s2=None, o1=None):
        if o1 is None:
            op("v", lambda: V.tensor_scalar(out, in0, s1, None, o0), r, w)
        else:
            op("v", lambda: V.tensor_scalar(out, in0, s1, s2, o0, o1), r, w)

    def vtt(out, a, b, r, w, alu):
        op("v", lambda: V.tensor_tensor(out, a, b, alu), r, w)

    def vcp(out, in_, r, w):
        op("v", lambda: V.tensor_copy(out, in_), r, w)

    def fill(out, pattern, base, w, cm=0):
        op("g", lambda: g.iota(out, pattern, base, cm, allow_small_or_imprecise_dtypes=True), "", w)

    def act(out, in_, r, w, func, bias=0.0, scale=1.0):
        op("s", lambda: S.activation(out, in_, func, bias=bias, scale=scale), r, w)

    def mms(out, pairs, r, w):
        def f():
            for i, (a, b) in enumerate(pairs):
                x = PE.matmul(out, a, b, i == 0, i == len(pairs) - 1)
            return x
        op("t", f, r, w)

    for k in range(3):
        dma("y", T.tb[:, 1024 * k:1024 * k + 1024], T.tab[:, 1024 * k:1024 * k + 1024], "ld%d" % k, "", "tb%d" % k)
    dma("s", T.ca[:], T.cx[:, :], "ld6", "", "caA caB")
    dma("s", T.vr[:, :], T.vv[:, :], "ld7", "", "vr")
    dma("s", T.dn[:, 384:576], T.tab[0::16, :], "ld3", "", "dnt")
    dma("s", T.dn[:, 0:192], T.suf[:, :], "ld4", "", "dnf")
    dma("s", T.dn[:, 192:384], T.lnk[:, :], "ld5", "", "dnl")

    PGC, PRC, PFC, P16, PM1, PP1, A1, A2, C15, WDc, WSc, WFc, R01, N15, D15, T1, T2, NPR, Q2, Q3, W2 = range(21)

    def col(i):
        return T.pc[:, i:i + 1]

    def key(i):
        return "pc%d" % i
    fill(T.iop[:], [[1, 1]], 0, "iop", 1)
    fill(col(PFC), [[1, 1]], 0, key(PFC), 1)
    fill(T.xf[:], [[1, 160]], 0, "xf")
    fill(T.xg[:], [[1, 8], [0, 16]], 0, "xg")
    fill(T.xr[:], [[0, 8], [1, 16]], 0, "xr")
    fill(T.ones[:], [[0, 512]], 1, "ones")
    GT = "gtx gt0 gt1 gt2 gt3"
    LT = "ltx lt0 lt1"
    fill(T.dtb[:, W0:WD], [[0, WD - W0]], 0, "dtx")
    fill(T.gt[:], [[0, WD]], 0, GT)
    fill(T.lt[:], [[0, WD]], -2, LT)
    fill(T.h0[:], [[0, 8]], 0, "h0")
    fill(T.inc[:, 0:8], [[0, 8]], 8191, "inc0")
    fill(T.zer[:], [[0, 96]], 0, "zer")
    for k in range(RO):
        fill(T["rb%d" % k][:, CAP:CAP + 16], [[0, 16]], 0, "rbx%d" % k)
    fill(T.tb[:, W0:WD], [[0, WD - W0]], 0, "tbx")
    fill(T.tm3[:], [[1, 128]], 0, "tm3")
    fill(T.pw[:, 0:CAP], [[0, CAP]], 0, "pw")

    vts(T.pi[:, 0:1], T.iop[:], "iop", "pi", 4, OP.arith_shift_right)
    vts(T.pi[:, 1:2], T.iop[:], "iop", "pi1", 15, OP.bitwise_and)
    vcp(col(PGC), T.pi[:, 0:1], "pi", key(PGC))
    vcp(col(PRC), T.pi[:, 1:2], "pi1", key(PRC))
    vts(T.oh16[:], T.xf[:, 0:16], "xf " + key(PRC), "oh16", col(PRC), OP.is_equal)

    def ohc(i):
        return T.oh16[:, i:i + 1]
    names = ["ida", "idb", "idc", "mdf", "mfl", "blk", "tri", "i14", "n8k", "e15", "moh", "mz0", "mz1", "nhf"]
    M = {n: T.mats[:, 128 * i:128 * i + 128] for i, n in enumerate(names)}
    M.update({n: T.sels[:, 160 * i:160 * i + 160] for i, n in enumerate(["selt", "seld", "selS", "selF", "vsel"])})
    xm = T.xf[:, 0:128]

    def mat(out, name, c, m, extra=""):
        vts(out, xm, "xf " + key(c) + " " + extra, name, col(c), OP.is_equal, m, OP.mult)

    def colop(i, src, srck, s1, o0, s2=None, o1=None):
        vts(col(i), src, srck, key(i), s1, o0, s2, o1)
    mat(M["ida"], "ida", PFC, 32.0)
    mat(M["idb"], "idb", PFC, 1.0)
    mat(M["idc"], "idc", PFC, EPS)
    vts(M["blk"], T.xg[:], "xg " + key(PGC), "blk", col(PGC), OP.is_equal)
    vts(T.m32[:], T.oh16[:], "oh16", "m32", -32.0, OP.mult)
    for r in range(16):
        act(T.expa[:, 128 * r:128 * r + 128], M["blk"], "blk m32", "expa%d" % r, AF.Copy, scale=T.m32[:, r:r + 1])
    EXPA = " ".join("expa%d" % r for r in range(16))
    colop(T1, col(PFC), key(PFC), 16.0, OP.mult, 16.0, OP.add)
    vts(M["vsel"], T.xf[:], "xf " + key(T1), "vsel", col(T1), OP.is_equal)
    colop(P16, col(PGC), key(PGC), 16.0, OP.mult, 16.0, OP.add)
    vts(M["selt"], T.xf[:], "xf " + key(P16), "selt", col(P16), OP.is_equal)
    vts(T.tm1[:], T.xr[:], "xr " + key(PRC), "tm1", col(PRC), OP.is_ge)
    vtt(M["tri"], T.tm1[:], M["blk"], "tm1 blk", "tri", OP.mult)
    colop(PM1, col(PFC), key(PFC), 1.0, OP.subtract)
    colop(A1, ohc(0), "oh16", -1.0 / 4096, OP.mult, 1.0 / 4096, OP.add)
    colop(A2, ohc(15), "oh16", 1.0 / 4096, OP.mult, -1.0 / 4096, OP.add)
    mat(T.tm1[:], "tm1", PM1, col(A1), key(A1))
    mat(T.tm2[:], "tm2", PFC, col(A2), key(A2))
    vtt(M["mdf"], T.tm1[:], T.tm2[:], "tm1 tm2", "mdf", OP.add)
    vts(M["mfl"], M["idb"], "idb oh16", "mfl", ohc(15), OP.mult, 0.25, OP.mult)
    colop(N15, ohc(15), "oh16", -1.0, OP.mult, 1.0, OP.add)
    colop(WDc, ohc(15), "oh16", 2.0 ** 19 - 4096.0, OP.mult, 4096.0, OP.add)
    colop(WSc, ohc(1), "oh16", 64.0, OP.mult, ohc(0), OP.add)
    colop(WFc, ohc(3), "oh16", 64.0, OP.mult, ohc(2), OP.add)
    for n, c in (("seld", WDc), ("selS", WSc), ("selF", WFc)):
        vts(M[n], T.xf[:], "xf " + key(P16) + " " + key(c), n, col(P16), OP.is_equal, col(c), OP.mult)
    colop(C15, ohc(15), "oh16", 2.0 ** 25, OP.mult)
    mat(M["i14"], "i14", PFC, 2.0 ** 14)
    vts(M["e15"], M["blk"], "blk " + key(C15), "e15", col(C15), OP.mult)

    pb = [0]

    def nextbank():
        pb[0] += 1
        return "b%d" % (pb[0] % 7)
    for k in range(3):
        c0 = 1024 * k
        cb, sg = ("cb", "sg") if k % 2 == 0 else ("cb2", "sg2")
        vts(T.ci[:], T.tb[:, c0:c0 + 1024], "tb%d" % k, "ci", 15, OP.bitwise_and)
        vcp(T[cb][:], T.ci[:], "ci", cb)
        act(T[sg][:], T[cb][:], cb, sg, AF.Sign)
        for h in range(2):
            p = slice(512 * h, 512 * h + 512)
            bk = nextbank()
            mms(T[bk][:], [(M["ida"], T[cb][:, p]), (M["idb"], T[sg][:, p]), (M["idc"], T[sg][:, p])], "ida idb idc " + cb + " " + sg, bk)
            act(T.kt[:, c0 + 512 * h:c0 + 512 * h + 512], T[bk][:], bk, "kt%d%d" % (k, h), AF.Copy, bias=-EPS)
    act(T.kt[:, W0:WD], T.dtb[:, W0:WD], "dtx", "ktx", AF.Copy, bias=-EPS)
    KT = "ktx " + " ".join("kt%d%d" % (k, h) for k in range(3) for h in range(2))
    DT = "dtx " + " ".join("dt%d%d" % (k, h) for k in range(3) for h in range(2))
    TB = "tbx tb0 tb1 tb2"

    def digits():
        q = 192
        vts(T.dg[:, 0:q], T.dn[:, 384:576], "dnt", "dg0", 4, OP.arith_shift_right, 63, OP.bitwise_and)
        vts(T.dg[:, q:2 * q], T.dn[:, 384:576], "dnt", "dg1", 10, OP.arith_shift_right)
        vts(T.dg[:, 2 * q:3 * q], T.dn[:, 0:192], "dnf", "dg2", 63, OP.bitwise_and)
        vts(T.dg[:, 3 * q:4 * q], T.dn[:, 0:192], "dnf", "dg3", 6, OP.arith_shift_right)
        vts(T.dg[:, 4 * q:5 * q], T.dn[:, 192:384], "dnl", "dg4", 63, OP.bitwise_and)
        vts(T.dg[:, 5 * q:6 * q], T.dn[:, 192:384], "dnl", "dg5", 6, OP.arith_shift_right)
        vcp(T.dgb[:, 0:4 * q], T.dg[:, 0:4 * q], "dg0 dg1 dg2 dg3", "dgb0")
        vts(T.dgb[:, 4 * q:6 * q], T.dg[:, 4 * q:6 * q], "dg4 dg5", "dgb1", -1.0, OP.mult, -2.0, OP.add)
        for k in range(4):
            dma("y", T.gt[k::16, 0:W0], T.dgb[:, k * q:k * q + q], "gd%d" % k, "dgb0", "gt%d" % k)
        for k in range(2):
            dma("y", T.lt[k::16, 0:W0], T.dgb[:, (4 + k) * q:(5 + k) * q], "gd%d" % (4 + k), "dgb1", "lt%d" % k)

    def pointers(k):
        c0 = 1024 * k
        vts(T.si[:], T.tb[:, c0:c0 + 1024], "tb%d" % k, "si", 4, OP.arith_shift_right)
        vts(T.s16[:], T.si[:], "si", "s16", 1792.0, OP.subtract)
        for h in range(2):
            p = slice(512 * h, 512 * h + 512)
            bk = "b%d" % (2 * (k % 2) + h)
            mms(T[bk][:], [(M["mdf"], T.s16[:, p]), (M["mfl"], T.ones[:])], "mdf mfl s16 ones", bk)
            vcp(T.rr[:, p], T[bk][:], bk, "rr%d" % h)
            vtt(T.dtb[:, c0 + 512 * h:c0 + 512 * h + 512], T[bk][:], T.rr[:, p], bk + " rr%d" % h, "dt%d%d" % (k, h), OP.subtract)
        if k == 0:
            vts(T.dtb[:, 0:1], T.dtb[:, 0:1], "dt00 " + key(N15), "dt00", col(N15), OP.mult)

    def late_constants():
        colop(PP1, col(PFC), key(PFC), 1.0, OP.add)
        colop(R01, ohc(0), "oh16", ohc(1), OP.add)
        colop(D15, ohc(15), "oh16", 10.25, OP.mult, -10.0, OP.add)
        colop(T2, col(PRC), key(PRC), 2560.0, OP.add)
        colop(NPR, col(PRC), key(PRC), -1.0, OP.mult)
        colop(Q2, ohc(2), "oh16", -1.0 / 32, OP.mult)
        colop(Q3, ohc(3), "oh16", -1.0 / 32, OP.mult)
        for t in range(RO - 1):
            colop(W2 + t, ohc(1), "oh16", 2.0 * t, OP.mult)
        act(T.jg[:], T.xf[:], "xf " + key(T2), "jg", AF.Identity, bias=col(T2), scale=16.0)
        for h in range(16):
            act(T.msk[:, h, :], T.xf[:, 0:16], "xf " + key(NPR), "msk%d" % h, AF.Relu, bias=col(NPR))
        for h in range(2):
            o = slice(8 * h, 8 * h + 8)
            vts(T.dja[:, o], T.jg[:, 0:8], "jg", "dja%d" % h, float(W - 2560 - 1792), OP.add, 32.0, OP.mult)
            vts(T.djb[:, o], T.jg[:, 0:8], "jg", "djb%d" % h, float(W - 2560), OP.add, -512.0, OP.mult)
        mat(M["n8k"], "n8k", PFC, -8192.0)
        mat(M["nhf"], "nhf", PFC, -0.5)
        mat(T.tm1[:], "tm1", PP1, col(N15), key(N15))
        mat(T.tm2[:], "tm2", PFC, col(N15), key(N15))
        vtt(M["moh"], T.tm1[:], T.tm2[:], "tm1 tm2", "moh", OP.subtract)
        mat(M["mz0"], "mz0", PFC, ohc(0), "oh16")
        mat(T.tm1[:], "tm1", PP1, ohc(0), "oh16")
        vtt(M["mz1"], T.tm1[:], M["mz0"], "tm1 mz0", "mz1", OP.add)
        vts(T.xi[:], T.tm3[:], "tm3", "xi", 63, OP.bitwise_and)
        vts(T.xs[:], T.tm3[:], "tm3", "xs", 6, OP.arith_shift_right)
        vts(T.tm1[:], T.xi[:], "xi oh16", "tm1", ohc(0), OP.mult)
        vts(T.tm2[:], T.xs[:], "xs oh16", "tm2", float(W0 // 64), OP.add, ohc(1), OP.mult)
        vtt(T.wdl[:], T.tm1[:], T.tm2[:], "tm1 tm2", "wdl", OP.add)

    def vlist(st):
        mms(T.b7[:, 352:512], [(M["vsel"][0:8, 16 - r:144 - r], T.vr[0:8, st * LN + r:(st + 1) * LN:16]) for r in range(16)], "vsel vr", "b7")
        act(T.v1[:, st * 160:st * 160 + 160], T.b7[:, 352:512], "b7", "v1_%d" % st, AF.Copy)
        act(T.v31[:, st * 160:st * 160 + 160], T.b7[:, 352:512], "b7", "v31_%d" % st, AF.Copy, scale=31.0)

    CUR = ["ca"]
    HCUR = ["h0"]
    for X in XS:
        vcp(T.cl[:, CQ[X]], T.ca[:, CQ[X]], "ca" + X, "cl" + X)

    def selmm(out, w, base, rhs, rk, start=True, stop=True):
        def f():
            for r in range(16):
                x = PE.matmul(out, M[base][:, 16 - r:144 - r], rhs[:, r::16], start and r == 0, stop and r == 15)
            return x
        op("t", f, base + " " + rk, w)

    def every(n, X):
        return " ".join(n + "b%d" % b for b in PIECES[X])

    def pieces(X):
        for i, b in enumerate(PIECES[X]):
            yield "b%d" % b, slice(512 * i, 512 * i + 512), slice(CQ[X].start + 32 * i, CQ[X].start + 32 * i + 32)

    TBANK = {"A": "b7", "B": "b6"}
    CBANK = {"A": "b5", "B": "b6"}
    CREG = {"A": T.b5[:, 0:96], "B": T.b6[:, 256:320]}
    LBANK = {"A": "b7", "B": "b6"}
    LREG = {"A": T.b7[:, 0:96], "B": T.b6[:, 320:384]}

    def counts(t, s, X):
        for bk, p, cq in pieces(X):
            kw = T.kt[:, 0:W0 + B * t].indirect(T.cl[:, cq])
            if t + s == 0:
                vcp(T["kap" + X][:, p], kw, KT + " cl" + X, "kap" + bk)
            else:
                vtt(T["kap" + X][:, p], kw, T["ne" + X][:, p], KT + " cl" + X + " ne" + bk, "kap" + bk, OP.mult)

    def total(X):
        selmm(T[TBANK[X]][:, 0:NQ[X]], TBANK[X], "selt", T["kap" + X], every("kap", X))

    def suffixes(t, X):
        act(T["gg" + X][:], T.gt[:, 0:W0 + B * t].indirect(T.cl[:, CQ[X]]), GT + " cl" + X, "gg" + X, AF.Copy)

    def targets(st, X):
        c = CQ[X]
        tk = TBANK[X]
        tp = T[tk][:, 0:NQ[X]]
        sc = slice(st * 160 + c.start, st * 160 + c.stop)
        vts(T.pp[:, c], tp, tk, "pp" + X, 1.0 / 32, OP.mult, 0.25, OP.subtract)
        vtt(T.vs[:, c], tp, T.v1[:, sc], tk + " v1_%d" % st, "vs" + X, OP.mult)
        vtt(T.wp[:, c], T.pp[:, c], T.v31[:, sc], "pp" + X + " v31_%d" % st, "wp" + X, OP.mult)
        vtt(T.vs[:, c], T.vs[:, c], T.wp[:, c], "vs" + X + " wp" + X, "vs" + X, OP.subtract)
        vts(T.qq[:, c], T.vs[:, c], "vs" + X, "qq" + X, 1.0 / 256, OP.mult, 1024.0 - 127.5 / 256, OP.add)

    def compare(X):
        for bk, p, cq in pieces(X):
            def f(bk=bk, p=p, cq=cq):
                PE.matmul(T[bk][:], M["tri"], T["kap" + X][:, p], True, False)
                for r in range(16):
                    x = PE.matmul(T[bk][:, r::16], T.expa[:, 128 * r:128 * r + 128], T.qq[:, cq], False, r == 15)
                return x
            op("t", f, "tri kap" + bk + " qq" + X + " " + EXPA, bk)
            act(T["cd" + X][:, p], T[bk][:], bk, "cd" + bk, AF.Sigmoid, bias=-16.0 * (32768 - 24), scale=-16.0)

    def suffix_sum(X):
        ap = T.b6[:, 64 + CQ[X].start:64 + CQ[X].stop]
        selmm(ap, "b6", "selF", T["gg" + X], "gg" + X)
        act(T.ff[:, CQ[X]], ap, "b6", "ff" + X, AF.Copy, bias=65536.0)

    def first_sum(X):
        selmm(CREG[X], CBANK[X], "selS", T["gg" + X], "gg" + X, True, False)

    def pointer(t, X):
        for bk, p, cq in pieces(X):
            vtt(T["ds" + X][:, p], T.dtb[:, 0:W0 + B * t].indirect(T.cl[:, cq]), T["cd" + X][:, p], DT + " cl" + X + " cd" + bk, "ds" + bk, OP.mult)

    def pointer_sum(X):
        selmm(CREG[X], CBANK[X], "seld", T["ds" + X], every("ds", X), False, True)

    def context(s, X, new):
        c = CQ[X]
        vtt(T.mm[:, c], CREG[X], T.ff[:, c], CBANK[X] + " ff" + X, "mm" + X, OP.min)
        if X == "A":
            vts(T.e8[:], T.b5[:, 0:8], "b5", "e8", 70000.0, OP.is_gt)
        if s == 1:
            vts(T.es[:, c], CREG[X], CBANK[X], "es" + X, 70000.0, OP.is_gt)
        vts(T[new][:, c], T.mm[:, c], "mm" + X, new + X, 4095, OP.bitwise_and)
        vcp(T.cl[:, c], T[new][:, c], new + X, "cl" + X)

    def mark_piece(s, X, bk, p):
        mms(T[bk][:], [(M["i14"], T["kap" + X][:, p]), (M["e15"], T["ds" + X][:, p])], "i14 e15 kap" + bk + " ds" + bk, bk)
        if s == 0:
            act(T["ne" + X][:, p], T[bk][:], bk, "ne" + bk, AF.Sigmoid, bias=256.0 * (2.0 ** 23 - 0.5), scale=-256.0)
        else:
            act(T["em" + X][:, p], T[bk][:], bk, "em" + bk, AF.Sign, bias=-(2.0 ** 23 - 0.5))

    def slots(X):
        c = CQ[X]
        ik = "inc0" if X == "A" else "incA"
        mms(T.b7[:, c], [(M["tri"], T.es[:, c]), (M["n8k"], T.es[:, c])], "tri n8k es" + X, "b7")
        mms(T.b6[:, 0:NQ[X]], [(M["blk"], T.es[:, c])], "blk es" + X, "b6")
        op("v", lambda: V.tensor_tensor_scan(T.inc[:, 8 + c.start:8 + c.stop], T.b6[:, 0:NQ[X]], T.zer[:, 0:NQ[X]], T.inc[:, 7 + c.start:8 + c.start], OP.add, OP.add), "b6 zer " + ik, "inc" + X)
        vtt(T.sa[:, c], T.inc[:, 7 + c.start:7 + c.stop], T.b7[:, c], "b7 inc" + X + " " + ik, "sa" + X, OP.add)
        vtt(T.sb2[:, c], T.sa[:, c], T.jg[:, c], "jg sa" + X, "sb" + X, OP.min)
        vcp(T.sl[:, c], T.sb2[:, c], "sb" + X, "sl" + X)
        vts(T.rl[:, c], T.sa[:, c], "sa" + X, "rl" + X, float(CAP), OP.min)

    def first_escape(old):
        hold = HCUR[0]
        hnew = "h1" if hold == "h0" else "h0"
        vts(T.ht[:], T[hold][:], hold, "ht", 0.0, OP.is_equal)
        vtt(T.ht[:], T.ht[:], T[old][:, 0:8], "ht " + old + "A", "ht", OP.mult)
        vtt(T.ht[:], T.ht[:], T[hold][:], "ht " + hold, "ht", OP.add)
        vtt(T[hnew][:], T.ht[:], T.e8[:], "ht e8", hnew, OP.mult)
        HCUR[0] = hnew

    def flip():
        old = CUR[0]
        CUR[0] = "cc" if old == "ca" else "ca"
        return old, CUR[0]

    def send(t):
        if t < RO - 1:
            vlist(SP * t + 2)
            vlist(SP * t + 3)
        for X in XS:
            for bk, p, cq in pieces(X):
                pwi = T.pw[:].indirect(T.sl[:, cq])
                if t < RO - 1:
                    vtt(pwi, T["gg" + X][:, p], T["em" + X][:, p], "sl" + X + " lg" + bk + " em" + bk, "pw", OP.mult)
                else:
                    vcp(pwi, T["gg" + X][:, p], "sl" + X + " lg" + bk, "pw")
        deps("g", ["pw"], [])
        dst = T.cores[(rank + 1) % len(T.cores)]
        src = T.cores[(rank - 1) % len(T.cores)]
        rid, pid, _se = topo.addr(dst)
        g.remote_dma(T["rb%d" % t][:, 0:CAP], T.pw[:, 0:CAP], T.sem["arr%d" % t], T.sem["snt%d" % t], pid, rid, topo.mask(core, dst))
        cnt["snt%d" % t] = len(topo.engines(core, dst))
        cnt["arr%d" % t] = len(topo.engines(src, core))
        mark(("rem", "snt%d" % t, cnt["snt%d" % t]), ["pw"], [])
        lw["rb%d" % t] = ("rem", "arr%d" % t, cnt["arr%d" % t])
        if t < RO - 1:
            fill(T.pw[:, 0:CAP], [[0, CAP]], 0, "pw")

    PEND = []

    def hop_recv(t):
        old, new = flip()
        PEND[:] = [old, new]
        RB = "rb%d rbx%d" % (t, t)
        win = T["rb%d" % t][:, 0:CAP + 16]
        for X in XS:
            ggk = "gg" + X + " " + every("lg", X)
            if t == RO - 1:
                act(T["gg" + X][:], win.indirect(T.rl[:, CQ[X]]), RB + " rl" + X, ggk, AF.Abs)
                selmm(LREG[X], LBANK[X], "selS", T["gg" + X], "gg" + X)
                continue
            act(T["cd" + X][:], win.indirect(T.rl[:, CQ[X]]), RB + " rl" + X, every("cd", X), AF.Copy)
            act(T["gg" + X][:], T["cd" + X][:], every("cd", X), ggk, AF.Abs)
            selmm(LREG[X], LBANK[X], "selS", T["gg" + X], "gg" + X)
            for bk, p, cq in pieces(X):
                mms(T[bk][:], [(M["idb"], T["cd" + X][:, p]), (M["nhf"], T["em" + X][:, p])], "idb nhf cd" + bk + " em" + bk, bk)
                act(T["ne" + X][:, p], T[bk][:], bk, "ne" + bk, AF.Sigmoid, scale=256.0)
        link_context(t, "A")
        if t == RO - 1:
            link_context(t, "B")
        else:
            h = HCUR[0]
            vtt(T[h][:], T[h][:], T.nr[:, 0:8], h + " nrA", h, OP.mult)

    def link_context(t, X):
        old, new = PEND
        c = CQ[X]
        vts(T.nr[:, c], LREG[X], LBANK[X], "nr" + X, 1.0, OP.is_lt)
        vts(T.rc[:, c], LREG[X], LBANK[X], "rc" + X, 130.0, OP.subtract, 0.0, OP.max)
        vtt(T.c1[:, c], T[old][:, c], T.nr[:, c], old + X + " nr" + X, "c1" + X, OP.mult)
        if t < RO - 1:
            vtt(T[new][:, c], T.c1[:, c], T.rc[:, c], "c1" + X + " rc" + X, new + X, OP.add)
            vcp(T.cl[:, c], T[new][:, c], new + X, "cl" + X)
        else:
            vtt(T.yo[:, c], T.c1[:, c], T.rc[:, c], "c1" + X + " rc" + X, "yo" + X, OP.add)

    def write_back(t, old, hb):
        full = t < RO - 1
        cur = CUR[0]
        wn = W0 + B * t
        wsl = slice(wn, wn + B)
        l8 = T.cl[:, 0:8]
        lf = T.fdu[:, 0:8]
        vts(T.cnd[:], T.e8[:], "e8", "cnd", 8192.0, OP.mult)
        vtt(T.cnd[:], T[hb][:], T.cnd[:], hb + " cnd", "cnd", OP.is_gt)
        vts(T.ka[:, 0:8], T[hb][:], hb, "ka0", 3840.0, OP.subtract)
        vts(T.ka[:, 8:16], T[old][:, 0:8], old + "A", "ka1", 3840.0, OP.subtract)
        vts(T.fdu[:], T.ka[:], "ka0 ka1", "fdu", 3840.0, OP.add)
        vtt(T.ka[:, 0:8], T.ka[:, 0:8], T.cnd[:], "ka0 cnd", "ka0", OP.mult)
        vtt(T.ka[:, 8:16], T.ka[:, 8:16], T.cnd[:], "ka1 cnd", "ka1", OP.mult)
        vts(T.k16[:, 0:16], T.ka[:], "ka0 ka1", "k16a", 2048.0, OP.add)
        vts(T.k32[:], T.ka[:], "ka0 ka1", "k32", 2048.0, OP.add, -32.0, OP.mult)
        nk = 16
        if full:
            nk = 32
            vts(T.dgi[:, 0:8], T[cur][:, 0:8], cur + "A", "dgi0", 63, OP.bitwise_and)
            vts(T.dgi[:, 8:16], T[cur][:, 0:8], cur + "A", "dgi1", 6, OP.arith_shift_right)
            vcp(T.k16[:, 16:32], T.dgi[:], "dgi0 dgi1", "k16b")

        def frow():
            for r in range(16):
                x = PE.matmul(T.b7[:, r:16 * nk:16], T.expa[:, 128 * r:128 * r + 128], T.k16[:, 0:nk], True, True)
            return x
        op("t", frow, EXPA + " k16a k16b", "b7")
        mms(T.b5[:, 0:B], [(M["moh"], T.cdA[:, 0:B]), (M["mz0"], T.ones[:, 0:B])], "moh cdb0 mz0 ones", "b5")
        act(T.ohf[:], T.b5[:, 0:B], "b5", "ohf", AF.Copy)
        act(T.oh3[:], T.b5[:, 0:B], "b5", "oh3", AF.Copy, scale=32.0)
        act(T.o33[:], T.b5[:, 0:B], "b5", "o33", AF.Copy, bias=-EPS, scale=33.0 + EPS)
        act(T.kf[:], T.kt[:, 0:wn].indirect(lf), KT + " fdu", "kf", AF.Copy)
        act(T.k2[:], T.kf[:], "kf", "k2", AF.Copy, bias=33.0, scale=-1.0)
        if full:
            act(T.xv[:], T.xf[:, 0:B], "xf", "xv", AF.Copy, bias=float(wn))
            act(T.wv[:], T.wdl[:], "wdl " + key(W2 + t), "wv", AF.Identity, bias=col(W2 + t))
            act(T.ohb[:], T.b5[:, 0:B], "b5", "ohb", AF.Copy)
            act(T.g1[:], T.gt[:, 0:wn].indirect(l8), GT + " clA " + key(R01), "g1", AF.Copy, scale=col(R01))
            act(T.gf[:], T.gt[:, 0:wn].indirect(lf), GT + " fdu", "gf", AF.Copy)
            act(T.lt[:, wsl], T.lt[:, 0:wn].indirect(l8), LT + " clA", LT, AF.Copy)
        for k in range(2):
            for p in range(8):
                i = 8 * k + p
                vts(T.eq[:, i, 0:B - 16 * p], T.b7[:, B * k + 16 * p:B * k + B], "b7 k32", "eq%d" % i, T.k32[:, i:i + 1], OP.is_equal)
        eqs = " ".join("eq%d" % i for i in range(16))
        vtt(T.eq[:, :, 0:16], T.eq[:, :, 0:16], T.msk[:, :, :], eqs + " " + " ".join("msk%d" % h for h in range(16)), eqs, OP.mult)
        vts(T.cr[:], T.b7[:, 0:256], "b7", "cr", -65536.0, OP.is_gt, 1.0, OP.subtract)
        if full:
            act(T.xt[:], T.b7[:, 256:384], "b7 " + key(Q2), "xt", AF.Copy, scale=col(Q2))
            act(T.xw[:], T.b7[:, 384:512], "b7 " + key(Q3), "xw", AF.Copy, scale=col(Q3))

        def fc():
            for k in range(2):
                for p in range(8):
                    x = PE.matmul(T.b6[:, B * k + 16 * p:B * k + B], M["blk"], T.eq[:, 8 * k + p, 0:B - 16 * p], p == 0, p == 7)
            return x
        op("t", fc, "blk " + eqs, "b6")
        dj = " dja0 dja1 djb0 djb1"
        vts(T.chi[:], T.kt[:, 0:wn].indirect(l8), KT + " clA", "chi", 1.0 / 64, OP.mult, 0.25, OP.add)
        vtt(T.fy[:], T.k32[:], T.dja[:], "k32" + dj, "fy", OP.add)
        vtt(T.k2[:], T.k2[:], T.ohf[:], "k2 ohf", "k2", OP.mult)
        vtt(T.kr[:], T.b6[:, 0:256], T.cr[:], "b6 cr", "kr", OP.is_le)
        selmm(T.b5[:, 128:144], "b5", "selt", T.kr, "kr")
        vtt(T.chf[:], T.chi[:], T.kr[:, 0:B], "chi kr", "chf", OP.mult)
        vts(T.cm[:], T.chf[:], "chf", "cm", 1.0, OP.min, 1.0 + EPS, OP.mult)
        vts(T.chf[:], T.chf[:], "chf", "chf", 32.0, OP.mult, EPS, OP.subtract)
        vtt(T.fy[:], T.b5[:, 128:144], T.fy[:], "b5 fy", "fy", OP.mult)
        vtt(T.fy[:], T.fy[:], T.djb[:], "fy" + dj, "fy", OP.add)
        vts(T.lw[:], T.fy[:], "fy", "lw", -1.0 / 512, OP.mult)
        vtt(T.kt[:, wsl], T.chf[:], T.cm[:], "chf cm", KT, OP.add)
        vtt(T.kt[:].indirect(T.lw[:, 0:8]), T.kf[:], T.k2[:], "kf k2 lw", KT, OP.add)
        if full:
            vcp(T.xi[:], T.tb[:, 0:wn].indirect(lf), TB + " fdu", "xi")
            vcp(T.tb[:, wsl], T.tb[:, 0:wn].indirect(l8), TB + " clA", TB)
            vts(T.dtb[:, wsl], T.dtb[:, 0:wn].indirect(l8), DT + " clA " + key(D15), DT, col(D15), OP.max)
            vts(T.xi[:], T.xi[:], "xi", "xi", 4, OP.arith_shift_right)
            vtt(T.xv[:], T.xv[:], T.xi[:], "xv xi", "xv", OP.subtract)
            vtt(T.xv[:], T.xv[:], T.ohf[:], "xv ohf", "xv", OP.mult)
            vtt(T.xv[:], T.xv[:], T.xi[:], "xv xi", "xv", OP.add)
            vts(T.s16[:, 0:B], T.xv[:], "xv", "s16", 1792.0, OP.subtract)
            mms(T.b5[:, 0:B], [(M["mdf"], T.s16[:, 0:B]), (M["mfl"], T.ones[:, 0:B])], "mdf mfl s16 ones", "b5")
            vts(T.xs[:], T.xv[:], "xv", "xs", 16.0, OP.mult)
            vcp(T.tb[:].indirect(T.lw[:, 0:8]), T.xs[:], "xs lw", TB)
        vtt(T.k2[:], T.kt[:, 0:wn].indirect(T.fdu[:, 8:16]), T.oh3[:], KT + " fdu oh3", "k2", OP.add)
        vts(T.k2[:], T.k2[:], "k2", "k2", 481.0, OP.min)
        vtt(T.kt[:].indirect(T.lw[:, 8:16]), T.k2[:], T.o33[:], "k2 o33 lw", KT, OP.max)
        if not full:
            return
        vcp(T.rr[:, 0:B], T.b5[:, 0:B], "b5", "rr0")
        vtt(T.xd[:], T.b5[:, 0:B], T.rr[:, 0:B], "b5 rr0", "xd", OP.subtract)
        vcp(T.dtb[:].indirect(T.lw[:, 0:8]), T.xd[:], "xd lw", DT)
        mms(T.b6[:, 0:B], [(M["mz1"], T.ohb[:])], "mz1 ohb", "b6")
        vtt(T.xt[:], T.xt[:], T.xw[:], "xt xw", "xt", OP.add)
        vtt(T.gt[:, wsl], T.xt[:], T.g1[:], "xt g1", GT, OP.add)
        vtt(T.wv[:], T.wv[:], T.gf[:], "wv gf", "wv", OP.subtract)
        vtt(T.g2[:], T.b6[:, 0:B], T.wv[:], "b6 wv", "g2", OP.mult)
        vtt(T.gt[:].indirect(T.lw[:, 0:8]), T.gf[:], T.g2[:], "gf g2 lw", GT, OP.add)

    for t in range(RO):
        for s in range(SP):
            st = SP * t + s
            if s == 0:
                if t == 0:
                    digits()
                    pointers(0)
                    vlist(0)
                    vlist(1)
                counts(t, 0, "A")
                total("A")
                if t > 0:
                    suffixes(t, "A")
                    link_context(t - 1, "B")
                else:
                    pointers(1)
                    suffixes(t, "A")
            targets(st, "A")
            compare("A")
            counts(t, s, "B")
            total("B")
            targets(st, "B")
            if st == 0:
                pointers(2)
            if s == 1:
                first_escape(old)
                hb = HCUR[0]
            compare("B")
            suffix_sum("A")
            first_sum("A")
            suffixes(t, "B")
            if st == 0:
                late_constants()
            pointer(t, "A")
            pointer(t, "B")
            old, new = flip()
            pointer_sum("A")
            context(s, "A", new)
            if s == 0:
                for bk, p, cq in pieces("A"):
                    mark_piece(0, "A", bk, p)
            suffix_sum("B")
            first_sum("B")
            pointer_sum("B")
            if s == 0:
                for bk, p, cq in pieces("B"):
                    mark_piece(0, "B", bk, p)
                counts(t, 1, "A")
                context(0, "B", new)
                total("A")
                suffixes(t, "A")
                continue
            for X in XS:
                if X == "B":
                    context(1, "B", new)
                slots(X)
                for bk, p, cq in pieces(X):
                    act(T["gg" + X][:, p], T.lt[:, 0:W0 + B * t].indirect(T.cl[:, cq]), LT + " cl" + X, "gg" + X + " lg" + bk, AF.Copy)
                    if t < RO - 1:
                        mark_piece(1, X, bk, p)
        send(t)
        if t < RO - 1:
            first_escape(old)
        write_back(t, old, hb)
        if t == RO - 1:
            for h in range(2):
                p = slice(W // 2 * h, W // 2 * (h + 1))
                act(T.ynb[:, p], T.kt[:, p], KT, "yn%d" % h, AF.Relu, bias=-1.0 / 32, scale=1.0 / 32)
                dma("y", T.yn[:, p], T.ynb[:, p], "ld%d" % (8 + h), "yn%d" % h, "")
        hop_recv(t)
    dma("y", T.yc[:, :], T.yo[:], "ld10", "yoA yoB", "")
    for s in sorted(cnt):
        need("g", s, cnt[s])
